import numpy as np
import ml_dtypes


def mxq(x, axis, fmt="e4m3"):
    dtype, down = {"e4m3": (ml_dtypes.float8_e4m3fn, 7), "e5m2": (ml_dtypes.float8_e5m2, 14)}[fmt]
    v = np.moveaxis(np.asarray(x, np.float32).astype(ml_dtypes.bfloat16).astype(np.float64), axis, -1)
    blocks = v.reshape(v.shape[:-1] + (-1, 32))
    amax = np.abs(blocks).max(-1, keepdims=True)
    byte = np.maximum(np.where(amax > 0, np.frexp(amax)[1] - 1 + 127, 0) - down, 1)
    scale = np.exp2(byte - 127.0)
    codes = (blocks / scale).astype(np.float32).astype(dtype).astype(np.float64)
    return np.moveaxis((codes * scale).reshape(v.shape), -1, axis)


WIDE = False


def mx_kscale(k):
    if not WIDE:
        return np.ones(k)
    levels = np.array([18, -18])
    if k % 512:
        return np.exp2(np.random.permutation(np.resize(levels, k // 32))).repeat(32)
    a = np.empty((k // 512, 16))
    for p in range(k // 512):
        a[p, :8] = np.random.permutation(np.resize(levels, 8))
        for g in range(8):
            far = levels[np.abs(levels - a[p, g]) >= 10]
            a[p, g + 8] = far[np.random.randint(len(far))]
    return np.exp2(a.ravel()).repeat(32)


def f64(x):
    return np.asarray(x).astype(np.float64)


def striped(idx):
    return np.tile(np.asarray(idx).reshape(-1, 16).T, (8, 1)).astype(np.uint16)


def unstriped(offs):
    return offs[:16].T.reshape(-1).astype(np.int64)


E2M1 = np.array([0.0, 0.5, 1.0, 1.5, 2.0, 3.0, 4.0, 6.0, -0.0, -0.5, -1.0, -1.5, -2.0, -3.0, -4.0, -6.0])


def pack_weight(w, fmt):
    k, n = w.shape
    w = f64(np.asarray(w, np.float32).astype(ml_dtypes.bfloat16)).reshape(k // 32, 32, n)
    amax = np.abs(w).max(1)
    if fmt == "e4m3":
        byte = np.frexp(amax)[1] - 1 + 127 - 7
    else:
        mant, ex = np.frexp(amax / 6.0)
        byte = np.where(mant > 0.5, ex, ex - 1) + 127
    byte = np.clip(np.where(amax > 0, byte, 1), 1, 254)
    scaled = (w * np.exp2(127.0 - byte)[:, None, :]).reshape(k, n).astype(np.float32)
    by_word = np.ascontiguousarray(scaled.reshape(k // 512, 128, 4, n).transpose(0, 1, 3, 2))
    if fmt == "e4m3":
        words = by_word.astype(ml_dtypes.float8_e4m3fn).view(np.uint8)
    else:
        c = by_word.astype(ml_dtypes.float4_e2m1fn).view(np.uint8) & 0xF
        words = (c[..., 0::2] | (c[..., 1::2] << 4)).reshape(k // 512, 128, 2 * n)
    return np.ascontiguousarray(words), np.ascontiguousarray(byte.astype(np.uint8).reshape(k // 512, 16, n))


def unpack_weight(words, scales, fmt):
    g, _, n = scales.shape
    words = np.ascontiguousarray(words).reshape(g, 128, n, -1)
    if fmt == "e4m3":
        vals = words.view(ml_dtypes.float8_e4m3fn).astype(np.float64)
    else:
        nib = np.empty((g, 128, n, 4), np.uint8)
        nib[..., 0::2] = words & 0xF
        nib[..., 1::2] = words >> 4
        vals = E2M1[nib]
    vals = vals * np.repeat(np.exp2(scales.astype(np.float64) - 127.0), 8, axis=1)[..., None]
    return vals.transpose(0, 1, 3, 2).reshape(g * 512, n)


B, N, T, D, R = 1, 512, 2048, 1024, 512


def setup_inputs():
    n = np.random.standard_normal
    idx = np.random.permutation(T)[:B * N]
    s = mx_kscale(D)[:, None]
    z = mx_kscale(R)[:, None]
    x = n((B, D, R))
    vp = pack_weight(n((D, T)) / np.sqrt(D) / s, "e2m1")
    return {
        "xT": (x * s).astype(np.float32),
        "wT": (n((D, T)) * (1.00 / np.sqrt(D)) / s).astype(np.float32),
        "v_words": np.ascontiguousarray(vp[0].reshape(1, 2, 128, T, 2).transpose(0, 2, 3, 1, 4)).reshape(1, 128, T, 4),
        "v_scales": vp[1],
        "wt": (np.random.uniform(0.5, 1.5, (B, R, 1)) * 1.0 / np.sqrt(R) * z).astype(np.float32),
        "xm": (x.transpose(0, 2, 1) / z).astype(np.float32),
        "offs": striped(idx),
    }


def reference(xT, wT, v_words, v_scales, wt, xm, offs):
    idx = unstriped(offs)
    v = unpack_weight(v_words.reshape(1, 128, T, 2, 2).transpose(0, 3, 1, 2, 4).reshape(2, 128, 2 * T), v_scales, "e2m1")
    pick = lambda x: x[:, idx].reshape(x.shape[0], B, N).transpose(1, 0, 2)
    xq = mxq(f64(xT), 1, "e4m3").transpose(0, 2, 1)
    a = xq @ mxq(pick(f64(wT)), 1, "e4m3")
    av = xq @ pick(v)
    g = f64(wt) * (a - av)
    dw = mxq(f64(xm), 1, "e4m3").transpose(0, 2, 1) @ mxq(g, 1, "e5m2")
    gw = np.zeros((D, T))
    gw[:, idx] = dw.transpose(1, 0, 2).reshape(D, B * N)
    return gw

@@ -1,0 +1,215 @@
+from contextlib import ExitStack
+
+import concourse.mybir as mybir
+
+N, T, D, R = 512, 2048, 1024, 512
+FLOPS = 3 * 2 * R * D * N
+
+F32 = mybir.dt.float32
+BF16 = mybir.dt.bfloat16
+I32 = mybir.dt.int32
+U32 = mybir.dt.uint32
+U16 = mybir.dt.uint16
+U8 = mybir.dt.uint8
+E4M3 = mybir.dt.float8_e4m3fn_x4
+E5M2 = mybir.dt.float8_e5m2_x4
+E2M1 = mybir.dt.float4_e2m1fn_x4
+COPY = mybir.ActivationFunctionType.Copy
+
+P = 128
+PACK = 4
+K_PASS = P * PACK
+PASSES = D // K_PASS
+WINDOWS = 3
+XM_PIECES = 4
+
+
+def tile_attend_gds_sq_kernel(tc, xT, wT, v_words, v_scales, wt, xm, offs, out):
+    nc = tc.nc
+    with ExitStack() as ctx:
+        sb = ctx.enter_context(tc.tile_pool(name="sb", bufs=1))
+        ps = ctx.enter_context(tc.psum_pool(name="ps", bufs=1))
+
+        def tile(name, shape, dtype, tag=None):
+            return sb.tile(shape, dtype, name=name, tag=tag or name, align_bytes=64)
+
+        offsets = sb.tile([P, N // 16], U16, name="offsets")
+        v_bytes = tile("v_bytes", [P, PASSES, T], U8)
+        nc.vector.memset(v_bytes[:].rearrange("p o t -> p (o t)").bitcast(I32), 0)
+
+        w_raw = [[tile(f"w_raw{g}{t}", [P, T], F32) for t in range(PACK)] for g in range(PASSES)]
+        x_rows = [xT[0, g * K_PASS : (g + 1) * K_PASS, :].rearrange("(p t) r -> p t r", t=PACK) for g in range(PASSES)]
+        wt_sb = tile("wt_sb", [P, PACK], F32)
+        x0_raw = tile("x0_raw", [P, PACK, R], F32)
+        for g in range(PASSES):
+            rows = wT[g * K_PASS : (g + 1) * K_PASS, :].rearrange("(p t) c -> p t c", t=PACK)
+            for t in range(PACK):
+                nc.sync.dma_start(out=w_raw[g][t][:], in_=rows[:, t, :])
+                if g == 0 and t == 0:
+                    nc.sync.dma_start(offsets[:], offs)
+                    nc.sync.dma_start(out=wt_sb[:], in_=wt[0].rearrange("(p t) o -> p (t o)", t=PACK))
+                    for q in range(4):
+                        nc.sync.dma_start(
+                            out=v_bytes[32 * q : 32 * q + 4, :, :].bitcast(I32),
+                            in_=v_scales[:, 4 * q : 4 * q + 4, :].rearrange("o f t -> f o t").bitcast(I32),
+                        )
+            if g == 0:
+                nc.sync.dma_start(out=x0_raw[:], in_=x_rows[0])
+        v_raw = tile("v_raw", [P, T], U32)
+        nc.sync.dma_start(out=v_raw[:].bitcast(I32), in_=v_words[0].rearrange("p t b -> p (t b)").bitcast(I32))
+        half = R // 2
+        x1_raw = [tile(f"x1_raw{h}", [P, PACK, half], F32) for h in range(2)]
+        for h in range(2):
+            nc.sync.dma_start(out=x1_raw[h][:], in_=x_rows[1][:, :, h * half : (h + 1) * half])
+        piece = D // XM_PIECES
+        xm_rows = xm[0].rearrange("(p t) d -> p t d", t=PACK)
+        xm_raw = [tile(f"xm_raw{c}", [P, PACK, piece], F32) for c in range(XM_PIECES)]
+        for c in range(XM_PIECES):
+            nc.sync.dma_start(out=xm_raw[c][:], in_=xm_rows[:, :, c * piece : (c + 1) * piece])
+
+        windows = [tile(f"window{j}", [P, T], F32) for j in range(WINDOWS)]
+        for window in windows:
+            nc.vector.memset(window[:].bitcast(I32), 0)
+        neg_wt = tile("neg_wt", [P, PACK], F32, tag="chain_d")
+        nc.vector.tensor_scalar_mul(neg_wt[:], wt_sb[:], -1.0)
+
+        def weave_views(dst, src):
+            return (
+                dst.rearrange("p (c i) t -> p c t i", i=4),
+                src.rearrange("p t (c i) -> p c t i", i=4),
+            )
+
+        def deal_views(woven, raw):
+            return (
+                woven.rearrange("p r s t -> p s t r"),
+                raw.rearrange("p t (s r) -> p s t r", r=PACK),
+            )
+
+        def gather_planes(g, tag):
+            planes = tile(f"w_planes{g}", [P, PACK, N], BF16, tag=tag)
+            for t in range(PACK):
+                nc.vector.tensor_copy(planes[:, t, :], w_raw[g][t][:].indirect(offsets[:]))
+            return planes
+
+        def weave_negated(g, planes, tag):
+            woven = tile(f"w_woven{g}", [P, N, PACK], BF16, tag=tag)
+            dst, src = weave_views(woven[:], planes[:])
+            nc.scalar.activation(dst, src, COPY, scale=-1.0)
+            return woven
+
+        def quantize(name, woven, width, fmt, tag=None):
+            codes = tile(f"{name}_codes", [P, width], U32, tag=tag)
+            scales = tile(f"{name}_scales", [P, width], U8)
+            nc.vector.quantize_mx(codes[:].bitcast(fmt), scales[:], woven)
+            return codes, scales
+
+        w_planes0 = gather_planes(0, "chain_a")
+        w_woven0 = weave_negated(0, w_planes0, "chain_b")
+        w0 = quantize("w0", w_woven0[:].rearrange("p n t -> p (n t)"), N, E4M3)
+
+        x_woven0 = tile("x_woven0", [P, PACK, P, PACK], BF16, tag="chain_a")
+        nc.scalar.copy(*deal_views(x_woven0[:], x0_raw[:]))
+
+        w_planes1 = gather_planes(1, "chain_b")
+        v_sc = [tile(f"v_sc{o}", [P, N], U8, tag=f"w_raw1{o}") for o in range(PASSES)]
+        for o in range(PASSES):
+            nc.vector.tensor_copy(v_sc[o][:], v_bytes[:, o, :].indirect(offsets[:]))
+        w_woven1 = weave_negated(1, w_planes1, "chain_c")
+        x0 = quantize("x0", x_woven0[:].rearrange("p r s t -> p (r s t)"), R, E4M3, tag="w_raw13")
+
+        scores = [ps.tile([P, N], F32, name=f"scores{r}") for r in range(PACK)]
+
+        def score_pass(r, x, rhs, rhs_scale, start, stop):
+            cols = slice(r * P, (r + 1) * P)
+            nc.tensor.matmul_mx(
+                scores[r][:],
+                lhsT=x[0][:, cols].bitcast(E4M3),
+                lhsT_scale=x[1][:, cols],
+                rhs=rhs,
+                rhs_scale=rhs_scale,
+                start=start,
+                stop=stop,
+            )
+
+        for r in range(PACK):
+            score_pass(r, x0, w0[0][:].bitcast(E4M3), w0[1][:], True, False)
+
+        v_pairs = tile("v_pairs", [P, N], U32, tag="chain_a")
+        nc.vector.tensor_copy(v_pairs[:], v_raw[:].indirect(offsets[:]))
+        v_codes = [tile(f"v_codes{o}", [P, 2 * N], U8) for o in range(PASSES)]
+        for o in range(PASSES):
+            nc.vector.tensor_copy(v_codes[o][:].bitcast(U16), v_pairs[:].bitcast(U16)[:, o::2])
+        for r in range(PACK):
+            score_pass(r, x0, v_codes[0][:].bitcast(E2M1), v_sc[0][:], False, False)
+        w1 = quantize("w1", w_woven1[:].rearrange("p n t -> p (n t)"), N, E4M3, tag="chain_a")
+
+        hp = P // 2
+        x_woven1 = [tile(f"x_woven1{h}", [P, PACK, hp, PACK], BF16, tag=("chain_b", "chain_c")[h]) for h in range(2)]
+        nc.scalar.copy(*deal_views(x_woven1[0][:], x1_raw[0][:]))
+        nc.vector.tensor_copy(*deal_views(x_woven1[1][:], x1_raw[1][:]))
+
+        x1 = (tile("x1_codes", [P, R], U32), tile("x1_scales", [P, R], U8))
+        for h in range(2):
+            for r in range(PACK):
+                cols = slice(r * P + h * hp, r * P + (h + 1) * hp)
+                nc.vector.quantize_mx(x1[0][:, cols].bitcast(E4M3), x1[1][:, cols], x_woven1[h][:, r, :, :].rearrange("p s t -> p (s t)"))
+
+        xm_q = {}
+
+        def xm_weave(c, copy, tag):
+            woven = tile(f"xm_woven{c}", [P, piece, PACK], BF16, tag=tag)
+            copy(*weave_views(woven[:], xm_raw[c][:]))
+            return woven
+
+        def xm_quantize(c, woven):
+            xm_q[c] = quantize(f"xm{c}", woven[:].rearrange("p d t -> p (d t)"), piece, E4M3)
+
+        xm_quantize(0, xm_weave(0, nc.vector.tensor_copy, "chain_c"))
+
+        g_planes = [tile(f"g_planes{u}", [P, 2, N], BF16) for u in range(2)]
+        g_woven = tile("g_woven", [P, N, PACK], BF16)
+        g_codes = tile("g_codes", [P, N], U32)
+        g_scales = tile("g_scales", [P, N], U8)
+        hn = N // 2
+        for r in range(PACK):
+            score_pass(r, x1, w1[0][:].bitcast(E4M3), w1[1][:], False, False)
+            score_pass(r, x1, v_codes[1][:].bitcast(E2M1), v_sc[1][:], False, True)
+            if r < PACK - 1:
+                nc.scalar.activation(g_planes[r // 2][:, r % 2, :], scores[r][:], COPY, scale=neg_wt[:, r : r + 1])
+            else:
+                for h in range(2):
+                    cols = slice(h * hn, (h + 1) * hn)
+                    nc.scalar.activation(g_planes[1][:, 1, cols], scores[r][:, cols], COPY, scale=neg_wt[:, r : r + 1])
+            if r == 1:
+                nc.vector.tensor_copy(g_woven[:, :, 0:2], g_planes[0][:].rearrange("p t n -> p n t"))
+        for h in range(2):
+            cols = slice(h * hn, (h + 1) * hn)
+            nc.vector.tensor_copy(g_woven[:, cols, 2:4], g_planes[1][:, :, cols].rearrange("p t n -> p n t"))
+        for h in range(2):
+            cols = slice(h * hn, (h + 1) * hn)
+            nc.vector.quantize_mx(g_codes[:, cols].bitcast(E5M2), g_scales[:, cols], g_woven[:, cols, :].rearrange("p n t -> p (n t)"))
+
+        xm_quantize(1, xm_weave(1, nc.scalar.copy, "chain_d"))
+        xm_quantize(2, xm_weave(2, nc.scalar.copy, None))
+
+        grads = [ps.tile([P, N], F32, name=f"grad{b}") for b in range(4)]
+        per_piece = piece // P
+        for j in range(D // P):
+            c, m = divmod(j, per_piece)
+            cols = slice(m * P, (m + 1) * P)
+            nc.tensor.matmul_mx(
+                grads[j % 4][:],
+                lhsT=xm_q[c][0][:, cols].bitcast(E4M3),
+                lhsT_scale=xm_q[c][1][:, cols],
+                rhs=g_codes[:].bitcast(E5M2),
+                rhs_scale=g_scales[:],
+                start=True,
+                stop=True,
+            )
+            dw = tile(f"dw{j}", [P, N], F32)
+            nc.scalar.copy(dw[:], grads[j % 4][:])
+            window = windows[j % WINDOWS]
+            nc.vector.tensor_copy(window[:].indirect(offsets[:]), dw[:])
+            nc.sync.dma_start(out=out[j * P : (j + 1) * P, :], in_=window[:])
+            if j == 0:
+                xm_quantize(3, xm_weave(3, nc.scalar.copy, "dw0"))

@@ -105,15 +105,15 @@ def tile_attend_gds_sq_kernel(tc, xT, wT, v_words, v_scales, wt, xm, offs, out):
 
         w_planes0 = gather_planes(0, "chain_a")
         w_woven0 = weave_negated(0, w_planes0, "chain_b")
+        v_sc = [tile(f"v_sc{o}", [P, N], U8, tag=f"w_raw0{3 - o}") for o in range(PASSES)]
+        for o in range(PASSES):
+            nc.vector.tensor_copy(v_sc[o][:], v_bytes[:, o, :].indirect(offsets[:]))
         w0 = quantize("w0", w_woven0[:].rearrange("p n t -> p (n t)"), N, E4M3)
 
         x_woven0 = tile("x_woven0", [P, PACK, P, PACK], BF16, tag="chain_a")
         nc.scalar.copy(*deal_views(x_woven0[:], x0_raw[:]))
 
         w_planes1 = gather_planes(1, "chain_b")
-        v_sc = [tile(f"v_sc{o}", [P, N], U8, tag=f"w_raw1{o}") for o in range(PASSES)]
-        for o in range(PASSES):
-            nc.vector.tensor_copy(v_sc[o][:], v_bytes[:, o, :].indirect(offsets[:]))
         w_woven1 = weave_negated(1, w_planes1, "chain_c")
         x0 = quantize("x0", x_woven0[:].rearrange("p r s t -> p (r s t)"), R, E4M3, tag="w_raw13")
 
@@ -189,8 +189,10 @@ def tile_attend_gds_sq_kernel(tc, xT, wT, v_words, v_scales, wt, xm, offs, out):
             cols = slice(h * hn, (h + 1) * hn)
             nc.vector.quantize_mx(g_codes[:, cols].bitcast(E5M2), g_scales[:, cols], g_woven[:, cols, :].rearrange("p n t -> p (n t)"))
 
-        xm_quantize(1, xm_weave(1, nc.scalar.copy, "chain_d"))
-        xm_quantize(2, xm_weave(2, nc.scalar.copy, None))
+        xm_woven1 = xm_weave(1, nc.scalar.copy, "chain_d")
+        xm_woven2 = xm_weave(2, nc.vector.tensor_copy, "g_woven")
+        xm_quantize(1, xm_woven1)
+        xm_quantize(2, xm_woven2)
 
         grads = [ps.tile([P, N], F32, name=f"grad{b}") for b in range(4)]
         per_piece = piece // P
@@ -207,9 +209,13 @@ def tile_attend_gds_sq_kernel(tc, xT, wT, v_words, v_scales, wt, xm, offs, out):
                 stop=True,
             )
             dw = tile(f"dw{j}", [P, N], F32)
-            nc.scalar.copy(dw[:], grads[j % 4][:])
             window = windows[j % WINDOWS]
-            nc.vector.tensor_copy(window[:].indirect(offsets[:]), dw[:])
+            parts = 2 if j == 0 else 1
+            width = N // parts
+            for h in range(parts):
+                slots = slice(h * width, (h + 1) * width)
+                nc.scalar.copy(dw[:, slots], grads[j % 4][:, slots])
+                nc.vector.tensor_copy(window[:].indirect(offsets[:, h * width // 16 : (h + 1) * width // 16]), dw[:, slots])
             nc.sync.dma_start(out=out[j * P : (j + 1) * P, :], in_=window[:])
             if j == 0:
                 xm_quantize(3, xm_weave(3, nc.scalar.copy, "dw0"))

@@ -36,11 +36,16 @@ def tile_attend_gds_sq_kernel(tc, xT, wT, v_words, v_scales, wt, xm, offs, out):
         offsets = sb.tile([P, N // 16], U16, name="offsets")
         v_bytes = tile("v_bytes", [P, PASSES, T], U8)
         nc.vector.memset(v_bytes[:].rearrange("p o t -> p (o t)").bitcast(I32), 0)
+        windows = [tile(f"window{j}", [P, T], F32) for j in range(WINDOWS)]
+        nc.vector.memset(windows[0][:].bitcast(I32), 0)
+        for window in windows[1:]:
+            nc.gpsimd.memset(window[:].bitcast(I32), 0)
 
         w_raw = [[tile(f"w_raw{g}{t}", [P, T], F32) for t in range(PACK)] for g in range(PASSES)]
+        x_raw = [tile(f"x_raw{g}", [P, PACK, R], F32) for g in range(PASSES)]
         x_rows = [xT[0, g * K_PASS : (g + 1) * K_PASS, :].rearrange("(p t) r -> p t r", t=PACK) for g in range(PASSES)]
         wt_sb = tile("wt_sb", [P, PACK], F32)
-        x0_raw = tile("x0_raw", [P, PACK, R], F32)
+        v_raw = tile("v_raw", [P, T], U32)
         for g in range(PASSES):
             rows = wT[g * K_PASS : (g + 1) * K_PASS, :].rearrange("(p t) c -> p t c", t=PACK)
             for t in range(PACK):
@@ -48,30 +53,23 @@ def tile_attend_gds_sq_kernel(tc, xT, wT, v_words, v_scales, wt, xm, offs, out):
                 if g == 0 and t == 0:
                     nc.sync.dma_start(offsets[:], offs)
                     nc.sync.dma_start(out=wt_sb[:], in_=wt[0].rearrange("(p t) o -> p (t o)", t=PACK))
-                    for q in range(4):
+                    for i in range(4):
                         nc.sync.dma_start(
-                            out=v_bytes[32 * q : 32 * q + 4, :, :].bitcast(I32),
-                            in_=v_scales[:, 4 * q : 4 * q + 4, :].rearrange("o f t -> f o t").bitcast(I32),
+                            out=v_bytes[i:P:32, :, :].bitcast(I32),
+                            in_=v_scales[:, i:16:4, :].rearrange("o f t -> f o t").bitcast(I32),
                         )
             if g == 0:
-                nc.sync.dma_start(out=x0_raw[:], in_=x_rows[0])
-        v_raw = tile("v_raw", [P, T], U32)
-        nc.sync.dma_start(out=v_raw[:].bitcast(I32), in_=v_words[0].rearrange("p t b -> p (t b)").bitcast(I32))
-        half = R // 2
-        x1_raw = [tile(f"x1_raw{h}", [P, PACK, half], F32) for h in range(2)]
-        for h in range(2):
-            nc.sync.dma_start(out=x1_raw[h][:], in_=x_rows[1][:, :, h * half : (h + 1) * half])
+                nc.sync.dma_start(out=x_raw[0][:], in_=x_rows[0])
+                nc.sync.dma_start(out=v_raw[:].bitcast(I32), in_=v_words[0].rearrange("p t b -> p (t b)").bitcast(I32))
+        nc.sync.dma_start(out=x_raw[1][:], in_=x_rows[1])
         piece = D // XM_PIECES
         xm_rows = xm[0].rearrange("(p t) d -> p t d", t=PACK)
         xm_raw = [tile(f"xm_raw{c}", [P, PACK, piece], F32) for c in range(XM_PIECES)]
         for c in range(XM_PIECES):
             nc.sync.dma_start(out=xm_raw[c][:], in_=xm_rows[:, :, c * piece : (c + 1) * piece])
 
-        windows = [tile(f"window{j}", [P, T], F32) for j in range(WINDOWS)]
-        for window in windows:
-            nc.vector.memset(window[:].bitcast(I32), 0)
-        neg_wt = tile("neg_wt", [P, PACK], F32, tag="chain_d")
-        nc.vector.tensor_scalar_mul(neg_wt[:], wt_sb[:], -1.0)
+        neg_wt = tile("neg_wt", [P, PACK], F32, tag="after_g")
+        nc.scalar.activation(neg_wt[:], wt_sb[:], COPY, scale=-1.0)
 
         def weave_views(dst, src):
             return (
@@ -79,20 +77,20 @@ def tile_attend_gds_sq_kernel(tc, xT, wT, v_words, v_scales, wt, xm, offs, out):
                 src.rearrange("p t (c i) -> p c t i", i=4),
             )
 
-        def deal_views(woven, raw):
+        def deal_views(woven, raw, first, count, cols=slice(0, P)):
             return (
-                woven.rearrange("p r s t -> p s t r"),
-                raw.rearrange("p t (s r) -> p s t r", r=PACK),
+                woven.rearrange("p r s t -> p s t r")[:, cols],
+                raw.rearrange("p t (s r) -> p s t r", r=PACK)[:, cols, :, first : first + count],
             )
 
-        def gather_planes(g, tag):
-            planes = tile(f"w_planes{g}", [P, PACK, N], BF16, tag=tag)
+        def gather_planes(g):
+            planes = tile(f"w_planes{g}", [P, PACK, N], BF16)
             for t in range(PACK):
                 nc.vector.tensor_copy(planes[:, t, :], w_raw[g][t][:].indirect(offsets[:]))
             return planes
 
-        def weave_negated(g, planes, tag):
-            woven = tile(f"w_woven{g}", [P, N, PACK], BF16, tag=tag)
+        def weave_negated(g, planes):
+            woven = tile(f"w_woven{g}", [P, N, PACK], BF16)
             dst, src = weave_views(woven[:], planes[:])
             nc.scalar.activation(dst, src, COPY, scale=-1.0)
             return woven
@@ -103,24 +101,43 @@ def tile_attend_gds_sq_kernel(tc, xT, wT, v_words, v_scales, wt, xm, offs, out):
             nc.vector.quantize_mx(codes[:].bitcast(fmt), scales[:], woven)
             return codes, scales
 
-        w_planes0 = gather_planes(0, "chain_a")
-        w_woven0 = weave_negated(0, w_planes0, "chain_b")
-        v_sc = [tile(f"v_sc{o}", [P, N], U8, tag=f"w_raw0{3 - o}") for o in range(PASSES)]
+        w_planes0 = gather_planes(0)
+        w_woven0 = weave_negated(0, w_planes0)
+        v_sc = [tile(f"v_sc{o}", [P, N], U8) for o in range(PASSES)]
         for o in range(PASSES):
             nc.vector.tensor_copy(v_sc[o][:], v_bytes[:, o, :].indirect(offsets[:]))
         w0 = quantize("w0", w_woven0[:].rearrange("p n t -> p (n t)"), N, E4M3)
 
-        x_woven0 = tile("x_woven0", [P, PACK, P, PACK], BF16, tag="chain_a")
-        nc.scalar.copy(*deal_views(x_woven0[:], x0_raw[:]))
+        x_woven0 = tile("x_woven0", [P, PACK, P, PACK], BF16)
+        nc.scalar.copy(*deal_views(x_woven0[:], x_raw[0][:], 0, PACK))
 
-        w_planes1 = gather_planes(1, "chain_b")
-        w_woven1 = weave_negated(1, w_planes1, "chain_c")
-        x0 = quantize("x0", x_woven0[:].rearrange("p r s t -> p (r s t)"), R, E4M3, tag="w_raw13")
+        v_pairs = tile("v_pairs", [P, N], U32)
+        nc.vector.tensor_copy(v_pairs[:], v_raw[:].indirect(offsets[:]))
+        v_codes = [tile(f"v_codes{o}", [P, 2 * N], U8) for o in range(PASSES)]
+        for o in range(PASSES):
+            nc.vector.tensor_copy(v_codes[o][:].bitcast(U16), v_pairs[:].bitcast(U16)[:, o::2])
+
+        hn = N // 2
+        halves = [slice(h * hn, (h + 1) * hn) for h in range(2)]
+        w_planes1 = tile("w_planes1", [P, PACK, N], BF16)
+        w_woven1 = tile("w_woven1", [P, N, PACK], BF16)
+        for t in range(PACK - 1):
+            nc.vector.tensor_copy(w_planes1[:, t, :], w_raw[1][t][:].indirect(offsets[:]))
+            if t == 1:
+                nc.scalar.activation(*weave_views(w_woven1[:, :, 0:2], w_planes1[:, 0:2, :]), COPY, scale=-1.0)
+        x0 = quantize("x0", x_woven0[:].rearrange("p r s t -> p (r s t)"), R, E4M3, tag="w_raw12")
+        for h in range(2):
+            nc.vector.tensor_copy(w_planes1[:, 3, halves[h]], w_raw[1][3][:].indirect(offsets[:, h * hn // 16 : (h + 1) * hn // 16]))
+        nc.scalar.activation(*weave_views(w_woven1[:, halves[0], 2:4], w_planes1[:, 2:4, halves[0]]), COPY, scale=-1.0)
+        nc.vector.tensor_scalar_mul(*weave_views(w_woven1[:, halves[1], 2:4], w_planes1[:, 2:4, halves[1]]), -1.0)
+        w1 = (tile("w1_codes", [P, N], U32), tile("w1_scales", [P, N], U8))
+        for cols in halves:
+            nc.vector.quantize_mx(w1[0][:, cols].bitcast(E4M3), w1[1][:, cols], w_woven1[:, cols, :].rearrange("p n t -> p (n t)"))
+
 
         scores = [ps.tile([P, N], F32, name=f"scores{r}") for r in range(PACK)]
 
-        def score_pass(r, x, rhs, rhs_scale, start, stop):
-            cols = slice(r * P, (r + 1) * P)
+        def score_pass(r, x, cols, rhs, rhs_scale, start, stop):
             nc.tensor.matmul_mx(
                 scores[r][:],
                 lhsT=x[0][:, cols].bitcast(E4M3),
@@ -132,27 +149,15 @@ def tile_attend_gds_sq_kernel(tc, xT, wT, v_words, v_scales, wt, xm, offs, out):
             )
 
         for r in range(PACK):
-            score_pass(r, x0, w0[0][:].bitcast(E4M3), w0[1][:], True, False)
+            score_pass(r, x0, slice(r * P, (r + 1) * P), w0[0][:].bitcast(E4M3), w0[1][:], True, False)
+            score_pass(r, x0, slice(r * P, (r + 1) * P), v_codes[0][:].bitcast(E2M1), v_sc[0][:], False, False)
 
-        v_pairs = tile("v_pairs", [P, N], U32, tag="chain_a")
-        nc.vector.tensor_copy(v_pairs[:], v_raw[:].indirect(offsets[:]))
-        v_codes = [tile(f"v_codes{o}", [P, 2 * N], U8) for o in range(PASSES)]
-        for o in range(PASSES):
-            nc.vector.tensor_copy(v_codes[o][:].bitcast(U16), v_pairs[:].bitcast(U16)[:, o::2])
-        for r in range(PACK):
-            score_pass(r, x0, v_codes[0][:].bitcast(E2M1), v_sc[0][:], False, False)
-        w1 = quantize("w1", w_woven1[:].rearrange("p n t -> p (n t)"), N, E4M3, tag="chain_a")
-
-        hp = P // 2
-        x_woven1 = [tile(f"x_woven1{h}", [P, PACK, hp, PACK], BF16, tag=("chain_b", "chain_c")[h]) for h in range(2)]
-        nc.scalar.copy(*deal_views(x_woven1[0][:], x1_raw[0][:]))
-        nc.vector.tensor_copy(*deal_views(x_woven1[1][:], x1_raw[1][:]))
-
-        x1 = (tile("x1_codes", [P, R], U32), tile("x1_scales", [P, R], U8))
-        for h in range(2):
-            for r in range(PACK):
-                cols = slice(r * P + h * hp, r * P + (h + 1) * hp)
-                nc.vector.quantize_mx(x1[0][:, cols].bitcast(E4M3), x1[1][:, cols], x_woven1[h][:, r, :, :].rearrange("p s t -> p (s t)"))
+        x_woven1 = [tile(f"x_woven1{u}", [P, 2, P, PACK], BF16) for u in range(2)]
+        x1 = []
+        for u, split in enumerate((64, 32)):
+            nc.vector.tensor_copy(*deal_views(x_woven1[u][:], x_raw[1][:], 2 * u, 2, slice(0, split)))
+            nc.scalar.copy(*deal_views(x_woven1[u][:], x_raw[1][:], 2 * u, 2, slice(split, P)))
+            x1.append(quantize(f"x1{u}", x_woven1[u][:].rearrange("p r s t -> p (r s t)"), 2 * P, E4M3))
 
         xm_q = {}
 
@@ -162,18 +167,18 @@ def tile_attend_gds_sq_kernel(tc, xT, wT, v_words, v_scales, wt, xm, offs, out):
             return woven
 
         def xm_quantize(c, woven):
-            xm_q[c] = quantize(f"xm{c}", woven[:].rearrange("p d t -> p (d t)"), piece, E4M3)
+            xm_q[c] = quantize(f"xm{c}", woven[:].rearrange("p d t -> p (d t)"), piece, E4M3, tag=f"xm{c}_codes")
 
-        xm_quantize(0, xm_weave(0, nc.vector.tensor_copy, "chain_c"))
+        xm_quantize(0, xm_weave(0, nc.vector.tensor_copy, "x_woven11"))
 
         g_planes = [tile(f"g_planes{u}", [P, 2, N], BF16) for u in range(2)]
         g_woven = tile("g_woven", [P, N, PACK], BF16)
         g_codes = tile("g_codes", [P, N], U32)
         g_scales = tile("g_scales", [P, N], U8)
-        hn = N // 2
         for r in range(PACK):
-            score_pass(r, x1, w1[0][:].bitcast(E4M3), w1[1][:], False, False)
-            score_pass(r, x1, v_codes[1][:].bitcast(E2M1), v_sc[1][:], False, True)
+            cols = slice(r % 2 * P, (r % 2 + 1) * P)
+            score_pass(r, x1[r // 2], cols, v_codes[1][:].bitcast(E2M1), v_sc[1][:], False, False)
+            score_pass(r, x1[r // 2], cols, w1[0][:].bitcast(E4M3), w1[1][:], False, True)
             if r < PACK - 1:
                 nc.scalar.activation(g_planes[r // 2][:, r % 2, :], scores[r][:], COPY, scale=neg_wt[:, r : r + 1])
             else:
@@ -189,10 +194,8 @@ def tile_attend_gds_sq_kernel(tc, xT, wT, v_words, v_scales, wt, xm, offs, out):
             cols = slice(h * hn, (h + 1) * hn)
             nc.vector.quantize_mx(g_codes[:, cols].bitcast(E5M2), g_scales[:, cols], g_woven[:, cols, :].rearrange("p n t -> p (n t)"))
 
-        xm_woven1 = xm_weave(1, nc.scalar.copy, "chain_d")
-        xm_woven2 = xm_weave(2, nc.vector.tensor_copy, "g_woven")
-        xm_quantize(1, xm_woven1)
-        xm_quantize(2, xm_woven2)
+
+        xm_quantize(1, xm_weave(1, nc.scalar.copy, "after_g"))
 
         grads = [ps.tile([P, N], F32, name=f"grad{b}") for b in range(4)]
         per_piece = piece // P
@@ -217,5 +220,5 @@ def tile_attend_gds_sq_kernel(tc, xT, wT, v_words, v_scales, wt, xm, offs, out):
                 nc.scalar.copy(dw[:, slots], grads[j % 4][:, slots])
                 nc.vector.tensor_copy(window[:].indirect(offsets[:, h * width // 16 : (h + 1) * width // 16]), dw[:, slots])
             nc.sync.dma_start(out=out[j * P : (j + 1) * P, :], in_=window[:])
-            if j == 0:
-                xm_quantize(3, xm_weave(3, nc.scalar.copy, "dw0"))
+            if m == per_piece - 1 and c + 2 < XM_PIECES:
+                xm_quantize(c + 2, xm_weave(c + 2, nc.scalar.copy, f"xm{c}_codes"))

@@ -37,9 +37,8 @@ def tile_attend_gds_sq_kernel(tc, xT, wT, v_words, v_scales, wt, xm, offs, out):
         v_bytes = tile("v_bytes", [P, PASSES, T], U8)
         nc.vector.memset(v_bytes[:].rearrange("p o t -> p (o t)").bitcast(I32), 0)
         windows = [tile(f"window{j}", [P, T], F32) for j in range(WINDOWS)]
-        nc.vector.memset(windows[0][:].bitcast(I32), 0)
-        for window in windows[1:]:
-            nc.gpsimd.memset(window[:].bitcast(I32), 0)
+        for window in windows:
+            nc.vector.memset(window[:].bitcast(I32), 0)
 
         w_raw = [[tile(f"w_raw{g}{t}", [P, T], F32) for t in range(PACK)] for g in range(PASSES)]
         x_raw = [tile(f"x_raw{g}", [P, PACK, R], F32) for g in range(PASSES)]

@@ -21,8 +21,7 @@ PACK = 4
 K_PASS = P * PACK
 PASSES = D // K_PASS
 WINDOWS = 3
-XM_PIECES = 4
-
+XM_WIDTHS = (256, 128, 128, 512)
 
 def tile_attend_gds_sq_kernel(tc, xT, wT, v_words, v_scales, wt, xm, offs, out):
     nc = tc.nc
@@ -36,39 +35,33 @@ def tile_attend_gds_sq_kernel(tc, xT, wT, v_words, v_scales, wt, xm, offs, out):
         offsets = sb.tile([P, N // 16], U16, name="offsets")
         v_bytes = tile("v_bytes", [P, PASSES, T], U8)
         nc.vector.memset(v_bytes[:].rearrange("p o t -> p (o t)").bitcast(I32), 0)
-        windows = [tile(f"window{j}", [P, T], F32) for j in range(WINDOWS)]
-        for window in windows:
-            nc.vector.memset(window[:].bitcast(I32), 0)
+        v_planes = tile("v_planes", [P, PASSES, N], U8)
+        nc.vector.memset(v_planes[:].rearrange("p o t -> p (o t)").bitcast(I32), 0)
 
         w_raw = [[tile(f"w_raw{g}{t}", [P, T], F32) for t in range(PACK)] for g in range(PASSES)]
+        w_rows = [wT[g * K_PASS : (g + 1) * K_PASS, :].rearrange("(p t) c -> p t c", t=PACK) for g in range(PASSES)]
         x_raw = [tile(f"x_raw{g}", [P, PACK, R], F32) for g in range(PASSES)]
         x_rows = [xT[0, g * K_PASS : (g + 1) * K_PASS, :].rearrange("(p t) r -> p t r", t=PACK) for g in range(PASSES)]
-        wt_sb = tile("wt_sb", [P, PACK], F32)
+        wt_sb = tile("wt_sb", [P, PACK], F32, tag="after_g")
         v_raw = tile("v_raw", [P, T], U32)
-        for g in range(PASSES):
-            rows = wT[g * K_PASS : (g + 1) * K_PASS, :].rearrange("(p t) c -> p t c", t=PACK)
-            for t in range(PACK):
-                nc.sync.dma_start(out=w_raw[g][t][:], in_=rows[:, t, :])
-                if g == 0 and t == 0:
-                    nc.sync.dma_start(offsets[:], offs)
-                    nc.sync.dma_start(out=wt_sb[:], in_=wt[0].rearrange("(p t) o -> p (t o)", t=PACK))
-                    for i in range(4):
-                        nc.sync.dma_start(
-                            out=v_bytes[i:P:32, :, :].bitcast(I32),
-                            in_=v_scales[:, i:16:4, :].rearrange("o f t -> f o t").bitcast(I32),
-                        )
-            if g == 0:
-                nc.sync.dma_start(out=x_raw[0][:], in_=x_rows[0])
-                nc.sync.dma_start(out=v_raw[:].bitcast(I32), in_=v_words[0].rearrange("p t b -> p (t b)").bitcast(I32))
-        nc.sync.dma_start(out=x_raw[1][:], in_=x_rows[1])
-        piece = D // XM_PIECES
-        xm_rows = xm[0].rearrange("(p t) d -> p t d", t=PACK)
-        xm_raw = [tile(f"xm_raw{c}", [P, PACK, piece], F32) for c in range(XM_PIECES)]
-        for c in range(XM_PIECES):
-            nc.sync.dma_start(out=xm_raw[c][:], in_=xm_rows[:, :, c * piece : (c + 1) * piece])
 
-        neg_wt = tile("neg_wt", [P, PACK], F32, tag="after_g")
-        nc.scalar.activation(neg_wt[:], wt_sb[:], COPY, scale=-1.0)
+        nc.sync.dma_start(out=w_raw[0][0][:], in_=w_rows[0][:, 0, :])
+        nc.sync.dma_start(offsets[:], offs)
+        nc.sync.dma_start(out=v_bytes[0:P:8, :, :].bitcast(I32), in_=v_scales.rearrange("o f t -> f o t").bitcast(I32))
+        for t in range(1, PACK):
+            nc.sync.dma_start(out=w_raw[0][t][:], in_=w_rows[0][:, t, :])
+        nc.sync.dma_start(out=x_raw[0][:], in_=x_rows[0])
+        nc.sync.dma_start(out=v_raw[:].bitcast(I32), in_=v_words[0].rearrange("p t b -> p (t b)").bitcast(I32))
+        for t in range(PACK):
+            nc.sync.dma_start(out=w_raw[1][t][:], in_=w_rows[1][:, t, :])
+        nc.sync.dma_start(out=x_raw[1][:], in_=x_rows[1])
+        nc.sync.dma_start(out=wt_sb[:], in_=wt[0].rearrange("(p t) o -> p (t o)", t=PACK))
+        xm_rows = xm[0].rearrange("(p t) d -> p t d", t=PACK)
+        xm_raw = []
+        for c, width in enumerate(XM_WIDTHS):
+            first = sum(XM_WIDTHS[:c])
+            xm_raw.append(tile(f"xm_raw{c}", [P, PACK, width], F32))
+            nc.sync.dma_start(out=xm_raw[c][:], in_=xm_rows[:, :, first : first + width])
 
         def weave_views(dst, src):
             return (
@@ -76,23 +69,11 @@ def tile_attend_gds_sq_kernel(tc, xT, wT, v_words, v_scales, wt, xm, offs, out):
                 src.rearrange("p t (c i) -> p c t i", i=4),
             )
 
-        def deal_views(woven, raw, first, count, cols=slice(0, P)):
+        def deal_views(woven, raw, first, count, cols):
             return (
                 woven.rearrange("p r s t -> p s t r")[:, cols],
                 raw.rearrange("p t (s r) -> p s t r", r=PACK)[:, cols, :, first : first + count],
             )
-
-        def gather_planes(g):
-            planes = tile(f"w_planes{g}", [P, PACK, N], BF16)
-            for t in range(PACK):
-                nc.vector.tensor_copy(planes[:, t, :], w_raw[g][t][:].indirect(offsets[:]))
-            return planes
-
-        def weave_negated(g, planes):
-            woven = tile(f"w_woven{g}", [P, N, PACK], BF16)
-            dst, src = weave_views(woven[:], planes[:])
-            nc.scalar.activation(dst, src, COPY, scale=-1.0)
-            return woven
 
         def quantize(name, woven, width, fmt, tag=None):
             codes = tile(f"{name}_codes", [P, width], U32, tag=tag)
@@ -100,15 +81,29 @@ def tile_attend_gds_sq_kernel(tc, xT, wT, v_words, v_scales, wt, xm, offs, out):
             nc.vector.quantize_mx(codes[:].bitcast(fmt), scales[:], woven)
             return codes, scales
 
-        w_planes0 = gather_planes(0)
-        w_woven0 = weave_negated(0, w_planes0)
-        v_sc = [tile(f"v_sc{o}", [P, N], U8) for o in range(PASSES)]
+        v_picked = tile("v_picked", [P, PASSES, N], U8)
         for o in range(PASSES):
-            nc.vector.tensor_copy(v_sc[o][:], v_bytes[:, o, :].indirect(offsets[:]))
-        w0 = quantize("w0", w_woven0[:].rearrange("p n t -> p (n t)"), N, E4M3)
+            nc.vector.tensor_copy(v_picked[:, o, :], v_bytes[:, o, :].indirect(offsets[:]))
+        for q in range(0, P, 32):
+            nc.scalar.dma_start(out=v_planes[q : q + 4, :, :].bitcast(I32), in_=v_picked[q : q + 32 : 8, :, :].bitcast(I32))
+
+        w_planes = [tile(f"w_planes{g}", [P, PACK, N], BF16) for g in range(PASSES)]
+        w_woven = [tile(f"w_woven{g}", [P, N, PACK], BF16) for g in range(PASSES)]
+        for t in range(PACK):
+            nc.vector.tensor_copy(w_planes[0][:, t, :], w_raw[0][t][:].indirect(offsets[:]))
+        nc.scalar.activation(*weave_views(w_woven[0][:], w_planes[0][:]), COPY, scale=-1.0)
+        w0 = quantize("w0", w_woven[0][:].rearrange("p n t -> p (n t)"), N, E4M3)
+        windows = [tile(f"window{j}", [P, T], F32) for j in range(WINDOWS)]
+        for window in windows:
+            nc.vector.memset(window[:].bitcast(I32), 0)
+
+        g_codes = tile("g_codes", [P, N], U32)
+        g_scales = tile("g_scales", [P, N], U8)
+        nc.vector.memset(g_codes[:, N // 2 :].bitcast(I32), 0)
+        nc.vector.memset(g_scales[:, N // 2 :].bitcast(I32), 0)
 
         x_woven0 = tile("x_woven0", [P, PACK, P, PACK], BF16)
-        nc.scalar.copy(*deal_views(x_woven0[:], x_raw[0][:], 0, PACK))
+        nc.scalar.copy(*deal_views(x_woven0[:], x_raw[0][:], 0, PACK, slice(0, P)))
 
         v_pairs = tile("v_pairs", [P, N], U32)
         nc.vector.tensor_copy(v_pairs[:], v_raw[:].indirect(offsets[:]))
@@ -118,21 +113,21 @@ def tile_attend_gds_sq_kernel(tc, xT, wT, v_words, v_scales, wt, xm, offs, out):
 
         hn = N // 2
         halves = [slice(h * hn, (h + 1) * hn) for h in range(2)]
-        w_planes1 = tile("w_planes1", [P, PACK, N], BF16)
-        w_woven1 = tile("w_woven1", [P, N, PACK], BF16)
         for t in range(PACK - 1):
-            nc.vector.tensor_copy(w_planes1[:, t, :], w_raw[1][t][:].indirect(offsets[:]))
+            nc.vector.tensor_copy(w_planes[1][:, t, :], w_raw[1][t][:].indirect(offsets[:]))
             if t == 1:
-                nc.scalar.activation(*weave_views(w_woven1[:, :, 0:2], w_planes1[:, 0:2, :]), COPY, scale=-1.0)
-        x0 = quantize("x0", x_woven0[:].rearrange("p r s t -> p (r s t)"), R, E4M3, tag="w_raw12")
+                nc.scalar.activation(*weave_views(w_woven[1][:, :, 0:2], w_planes[1][:, 0:2, :]), COPY, scale=-1.0)
+        x0 = (tile("x0_codes", [P, R], U32, tag="w_raw12"), tile("x0_scales", [P, R], U8))
+        for u in range(2):
+            cols = slice(2 * u * P, 2 * (u + 1) * P)
+            nc.vector.quantize_mx(x0[0][:, cols].bitcast(E4M3), x0[1][:, cols], x_woven0[:, 2 * u : 2 * u + 2].rearrange("p r s t -> p (r s t)"))
         for h in range(2):
-            nc.vector.tensor_copy(w_planes1[:, 3, halves[h]], w_raw[1][3][:].indirect(offsets[:, h * hn // 16 : (h + 1) * hn // 16]))
-        nc.scalar.activation(*weave_views(w_woven1[:, halves[0], 2:4], w_planes1[:, 2:4, halves[0]]), COPY, scale=-1.0)
-        nc.vector.tensor_scalar_mul(*weave_views(w_woven1[:, halves[1], 2:4], w_planes1[:, 2:4, halves[1]]), -1.0)
+            nc.vector.tensor_copy(w_planes[1][:, 3, halves[h]], w_raw[1][3][:].indirect(offsets[:, h * hn // 16 : (h + 1) * hn // 16]))
+        nc.scalar.activation(*weave_views(w_woven[1][:, halves[0], 2:4], w_planes[1][:, 2:4, halves[0]]), COPY, scale=-1.0)
+        nc.vector.tensor_scalar_mul(*weave_views(w_woven[1][:, halves[1], 2:4], w_planes[1][:, 2:4, halves[1]]), -1.0)
         w1 = (tile("w1_codes", [P, N], U32), tile("w1_scales", [P, N], U8))
         for cols in halves:
-            nc.vector.quantize_mx(w1[0][:, cols].bitcast(E4M3), w1[1][:, cols], w_woven1[:, cols, :].rearrange("p n t -> p (n t)"))
-
+            nc.vector.quantize_mx(w1[0][:, cols].bitcast(E4M3), w1[1][:, cols], w_woven[1][:, cols, :].rearrange("p n t -> p (n t)"))
 
         scores = [ps.tile([P, N], F32, name=f"scores{r}") for r in range(PACK)]
 
@@ -149,75 +144,80 @@ def tile_attend_gds_sq_kernel(tc, xT, wT, v_words, v_scales, wt, xm, offs, out):
 
         for r in range(PACK):
             score_pass(r, x0, slice(r * P, (r + 1) * P), w0[0][:].bitcast(E4M3), w0[1][:], True, False)
-            score_pass(r, x0, slice(r * P, (r + 1) * P), v_codes[0][:].bitcast(E2M1), v_sc[0][:], False, False)
+            score_pass(r, x0, slice(r * P, (r + 1) * P), v_codes[0][:].bitcast(E2M1), v_planes[:, 0, :], False, False)
 
-        x_woven1 = [tile(f"x_woven1{u}", [P, 2, P, PACK], BF16) for u in range(2)]
+        hp = P // 2
+        x1_view = x_raw[1][:].rearrange("p t (s r) -> p s t r", r=PACK)
         x1 = []
-        for u, split in enumerate((64, 32)):
-            nc.vector.tensor_copy(*deal_views(x_woven1[u][:], x_raw[1][:], 2 * u, 2, slice(0, split)))
-            nc.scalar.copy(*deal_views(x_woven1[u][:], x_raw[1][:], 2 * u, 2, slice(split, P)))
-            x1.append(quantize(f"x1{u}", x_woven1[u][:].rearrange("p r s t -> p (r s t)"), 2 * P, E4M3))
+        for u in range(2):
+            codes, scales = tile(f"x1{u}_codes", [P, 2 * P], U32), tile(f"x1{u}_scales", [P, 2 * P], U8)
+            low = tile(f"x1{u}_low", [P, 2, hp, PACK], BF16, tag=("x10_low", "x10_high")[u])
+            high = tile(f"x1{u}_high", [P, 2, hp, PACK], BF16)
+            nc.vector.tensor_copy(low[:].rearrange("p r s t -> p s t r"), x1_view[:, 0:hp, :, 2 * u : 2 * u + 2])
+            nc.scalar.copy(high[:].rearrange("p r s t -> p s t r"), x1_view[:, hp:P, :, 2 * u : 2 * u + 2])
+            for r in range(2):
+                for h, woven in enumerate((low, high)):
+                    cols = slice(r * P + h * hp, r * P + (h + 1) * hp)
+                    nc.vector.quantize_mx(codes[:, cols].bitcast(E4M3), scales[:, cols], woven[:, r].rearrange("p s t -> p (s t)"))
+            x1.append((codes, scales))
 
-        xm_q = {}
+        xm_q = []
 
-        def xm_weave(c, copy, tag):
-            woven = tile(f"xm_woven{c}", [P, piece, PACK], BF16, tag=tag)
+        def xm_prepare(c, copy, tag):
+            width = XM_WIDTHS[c]
+            woven = tile(f"xm_woven{c}", [P, width, PACK], BF16, tag=tag)
             copy(*weave_views(woven[:], xm_raw[c][:]))
-            return woven
+            codes, scales = quantize(f"xm{c}", woven[:].rearrange("p d t -> p (d t)"), width, E4M3)
+            xm_q.extend((c, codes[:, m : m + P], scales[:, m : m + P]) for m in range(0, width, P))
 
-        def xm_quantize(c, woven):
-            xm_q[c] = quantize(f"xm{c}", woven[:].rearrange("p d t -> p (d t)"), piece, E4M3, tag=f"xm{c}_codes")
-
-        xm_quantize(0, xm_weave(0, nc.vector.tensor_copy, "x_woven11"))
+        xm_prepare(0, nc.vector.tensor_copy, "x11_high")
 
         g_planes = [tile(f"g_planes{u}", [P, 2, N], BF16) for u in range(2)]
         g_woven = tile("g_woven", [P, N, PACK], BF16)
-        g_codes = tile("g_codes", [P, N], U32)
-        g_scales = tile("g_scales", [P, N], U8)
         for r in range(PACK):
             cols = slice(r % 2 * P, (r % 2 + 1) * P)
-            score_pass(r, x1[r // 2], cols, v_codes[1][:].bitcast(E2M1), v_sc[1][:], False, False)
+            score_pass(r, x1[r // 2], cols, v_codes[1][:].bitcast(E2M1), v_planes[:, 1, :], False, False)
             score_pass(r, x1[r // 2], cols, w1[0][:].bitcast(E4M3), w1[1][:], False, True)
-            if r < PACK - 1:
-                nc.scalar.activation(g_planes[r // 2][:, r % 2, :], scores[r][:], COPY, scale=neg_wt[:, r : r + 1])
-            else:
-                for h in range(2):
-                    cols = slice(h * hn, (h + 1) * hn)
-                    nc.scalar.activation(g_planes[1][:, 1, cols], scores[r][:, cols], COPY, scale=neg_wt[:, r : r + 1])
+            for cols in halves if r == PACK - 1 else [slice(0, N)]:
+                nc.scalar.activation(g_planes[r // 2][:, r % 2, cols], scores[r][:, cols], COPY, scale=wt_sb[:, r : r + 1])
             if r == 1:
-                nc.vector.tensor_copy(g_woven[:, :, 0:2], g_planes[0][:].rearrange("p t n -> p n t"))
-        for h in range(2):
-            cols = slice(h * hn, (h + 1) * hn)
-            nc.vector.tensor_copy(g_woven[:, cols, 2:4], g_planes[1][:, :, cols].rearrange("p t n -> p n t"))
-        for h in range(2):
-            cols = slice(h * hn, (h + 1) * hn)
-            nc.vector.quantize_mx(g_codes[:, cols].bitcast(E5M2), g_scales[:, cols], g_woven[:, cols, :].rearrange("p n t -> p (n t)"))
-
-
-        xm_quantize(1, xm_weave(1, nc.scalar.copy, "after_g"))
+                for cols in halves:
+                    nc.vector.tensor_copy(g_woven[:, cols, 0:2], g_planes[0][:, :, cols].rearrange("p t n -> p n t"))
 
         grads = [ps.tile([P, N], F32, name=f"grad{b}") for b in range(4)]
-        per_piece = piece // P
-        for j in range(D // P):
-            c, m = divmod(j, per_piece)
-            cols = slice(m * P, (m + 1) * P)
+        dws = [tile(f"dw{j}", [P, N], F32) for j in range(D // P)]
+
+        def finish_g(cols):
+            nc.vector.tensor_copy(g_woven[:, cols, 2:4], g_planes[1][:, :, cols].rearrange("p t n -> p n t"))
+            nc.vector.quantize_mx(g_codes[:, cols].bitcast(E5M2), g_scales[:, cols], g_woven[:, cols, :].rearrange("p n t -> p (n t)"))
+
+        def gradient(j, bank, slots):
+            c, codes, scales = xm_q[j]
             nc.tensor.matmul_mx(
-                grads[j % 4][:],
-                lhsT=xm_q[c][0][:, cols].bitcast(E4M3),
-                lhsT_scale=xm_q[c][1][:, cols],
+                bank[:],
+                lhsT=codes.bitcast(E4M3),
+                lhsT_scale=scales,
                 rhs=g_codes[:].bitcast(E5M2),
                 rhs_scale=g_scales[:],
                 start=True,
                 stop=True,
             )
-            dw = tile(f"dw{j}", [P, N], F32)
-            window = windows[j % WINDOWS]
-            parts = 2 if j == 0 else 1
-            width = N // parts
-            for h in range(parts):
-                slots = slice(h * width, (h + 1) * width)
-                nc.scalar.copy(dw[:, slots], grads[j % 4][:, slots])
-                nc.vector.tensor_copy(window[:].indirect(offsets[:, h * width // 16 : (h + 1) * width // 16]), dw[:, slots])
-            nc.sync.dma_start(out=out[j * P : (j + 1) * P, :], in_=window[:])
-            if m == per_piece - 1 and c + 2 < XM_PIECES:
-                xm_quantize(c + 2, xm_weave(c + 2, nc.scalar.copy, f"xm{c}_codes"))
+            nc.scalar.activation(dws[j][:, slots], bank[:, slots], COPY, scale=-1.0)
+
+        def scatter(j, slots):
+            entries = offsets[:, slots.start // 16 : slots.stop // 16]
+            nc.vector.tensor_copy(windows[j % WINDOWS][:].indirect(entries), dws[j][:, slots])
+
+        finish_g(halves[0])
+        gradient(0, grads[3], halves[0])
+        finish_g(halves[1])
+        xm_prepare(1, nc.scalar.copy, "after_g")
+        scatter(0, halves[0])
+        for j in range(D // P):
+            slots = halves[1] if j == 0 else slice(0, N)
+            gradient(j, grads[j % 4], slots)
+            scatter(j, slots)
+            nc.sync.dma_start(out=out[j * P : (j + 1) * P, :], in_=windows[j % WINDOWS][:])
+            c = xm_q[j][0]
+            if c + 2 < len(XM_WIDTHS) and xm_q[j + 1][0] != c:
+                xm_prepare(c + 2, nc.scalar.copy, f"xm{c}_codes")

@@ -15,13 +15,20 @@ E4M3 = mybir.dt.float8_e4m3fn_x4
 E5M2 = mybir.dt.float8_e5m2_x4
 E2M1 = mybir.dt.float4_e2m1fn_x4
 COPY = mybir.ActivationFunctionType.Copy
+MULT = mybir.AluOpType.mult
+ADD = mybir.AluOpType.add
 
 P = 128
 PACK = 4
 K_PASS = P * PACK
 PASSES = D // K_PASS
 WINDOWS = 3
-XM_WIDTHS = (256, 128, 128, 512)
+QUARTERS = N // P
+HALF = N // 2
+LEAD = N - P
+EARLY = 2
+XM_WIDTHS = (128, 128, 128, 128, 512)
+
 
 def tile_attend_gds_sq_kernel(tc, xT, wT, v_words, v_scales, wt, xm, offs, out):
     nc = tc.nc
@@ -33,6 +40,12 @@ def tile_attend_gds_sq_kernel(tc, xT, wT, v_words, v_scales, wt, xm, offs, out):
             return sb.tile(shape, dtype, name=name, tag=tag or name, align_bytes=64)
 
         offsets = sb.tile([P, N // 16], U16, name="offsets")
+        halves = [slice(h * HALF, (h + 1) * HALF) for h in range(2)]
+        quarters = [slice(q * P, (q + 1) * P) for q in range(QUARTERS)]
+
+        def entries(slots):
+            return offsets[:, slots.start // 16 : slots.stop // 16]
+
         v_bytes = tile("v_bytes", [P, PASSES, T], U8)
         nc.vector.memset(v_bytes[:].rearrange("p o t -> p (o t)").bitcast(I32), 0)
         v_planes = tile("v_planes", [P, PASSES, N], U8)
@@ -42,7 +55,7 @@ def tile_attend_gds_sq_kernel(tc, xT, wT, v_words, v_scales, wt, xm, offs, out):
         w_rows = [wT[g * K_PASS : (g + 1) * K_PASS, :].rearrange("(p t) c -> p t c", t=PACK) for g in range(PASSES)]
         x_raw = [tile(f"x_raw{g}", [P, PACK, R], F32) for g in range(PASSES)]
         x_rows = [xT[0, g * K_PASS : (g + 1) * K_PASS, :].rearrange("(p t) r -> p t r", t=PACK) for g in range(PASSES)]
-        wt_sb = tile("wt_sb", [P, PACK], F32, tag="after_g")
+        wt_sb = tile("wt_sb", [P, PACK], F32)
         v_raw = tile("v_raw", [P, T], U32)
 
         nc.sync.dma_start(out=w_raw[0][0][:], in_=w_rows[0][:, 0, :])
@@ -50,10 +63,10 @@ def tile_attend_gds_sq_kernel(tc, xT, wT, v_words, v_scales, wt, xm, offs, out):
         nc.sync.dma_start(out=v_bytes[0:P:8, :, :].bitcast(I32), in_=v_scales.rearrange("o f t -> f o t").bitcast(I32))
         for t in range(1, PACK):
             nc.sync.dma_start(out=w_raw[0][t][:], in_=w_rows[0][:, t, :])
-        nc.sync.dma_start(out=x_raw[0][:], in_=x_rows[0])
-        nc.sync.dma_start(out=v_raw[:].bitcast(I32), in_=v_words[0].rearrange("p t b -> p (t b)").bitcast(I32))
         for t in range(PACK):
             nc.sync.dma_start(out=w_raw[1][t][:], in_=w_rows[1][:, t, :])
+        nc.sync.dma_start(out=x_raw[0][:], in_=x_rows[0])
+        nc.sync.dma_start(out=v_raw[:].bitcast(I32), in_=v_words[0].rearrange("p t b -> p (t b)").bitcast(I32))
         nc.sync.dma_start(out=x_raw[1][:], in_=x_rows[1])
         nc.sync.dma_start(out=wt_sb[:], in_=wt[0].rearrange("(p t) o -> p (t o)", t=PACK))
         xm_rows = xm[0].rearrange("(p t) d -> p t d", t=PACK)
@@ -69,10 +82,10 @@ def tile_attend_gds_sq_kernel(tc, xT, wT, v_words, v_scales, wt, xm, offs, out):
                 src.rearrange("p t (c i) -> p c t i", i=4),
             )
 
-        def deal_views(woven, raw, first, count, cols):
+        def deal_views(woven, raw, first, count):
             return (
-                woven.rearrange("p r s t -> p s t r")[:, cols],
-                raw.rearrange("p t (s r) -> p s t r", r=PACK)[:, cols, :, first : first + count],
+                woven.rearrange("p r (c e) t -> p c t e r", e=2),
+                raw.rearrange("p t (c e r) -> p c t e r", e=2, r=PACK)[:, :, :, :, first : first + count],
             )
 
         def quantize(name, woven, width, fmt, tag=None):
@@ -87,53 +100,63 @@ def tile_attend_gds_sq_kernel(tc, xT, wT, v_words, v_scales, wt, xm, offs, out):
         for q in range(0, P, 32):
             nc.scalar.dma_start(out=v_planes[q : q + 4, :, :].bitcast(I32), in_=v_picked[q : q + 32 : 8, :, :].bitcast(I32))
 
-        w_planes = [tile(f"w_planes{g}", [P, PACK, N], BF16) for g in range(PASSES)]
-        w_woven = [tile(f"w_woven{g}", [P, N, PACK], BF16) for g in range(PASSES)]
-        for t in range(PACK):
-            nc.vector.tensor_copy(w_planes[0][:, t, :], w_raw[0][t][:].indirect(offsets[:]))
-        nc.scalar.activation(*weave_views(w_woven[0][:], w_planes[0][:]), COPY, scale=-1.0)
-        w0 = quantize("w0", w_woven[0][:].rearrange("p n t -> p (n t)"), N, E4M3)
+        w = []
         windows = [tile(f"window{j}", [P, T], F32) for j in range(WINDOWS)]
-        for window in windows:
-            nc.vector.memset(window[:].bitcast(I32), 0)
+        for g in range(PASSES):
+            planes = tile(f"w_planes{g}", [P, PACK, N], BF16)
+            woven = [tile(f"w_woven{g}{h}", [P, HALF, PACK], BF16) for h in range(2)]
+            for t in range(PACK):
+                nc.vector.tensor_copy(planes[:, t, :], w_raw[g][t][:].indirect(offsets[:]))
+                if g == 0 and t > 0:
+                    nc.vector.memset(windows[t - 1][:].bitcast(I32), 0)
+            nc.scalar.activation(*weave_views(woven[0][:], planes[:, :, halves[0]]), COPY, scale=-1.0)
+            nc.vector.tensor_scalar_mul(*weave_views(woven[1][:], planes[:, :, halves[1]]), -1.0)
+            w.append(woven)
 
-        g_codes = tile("g_codes", [P, N], U32)
-        g_scales = tile("g_scales", [P, N], U8)
-        nc.vector.memset(g_codes[:, N // 2 :].bitcast(I32), 0)
-        nc.vector.memset(g_scales[:, N // 2 :].bitcast(I32), 0)
+        g_codes = tile("g_codes", [P, LEAD + N], U32)
+        g_scales = tile("g_scales", [P, LEAD + N], U8)
+        nc.vector.memset(g_codes[:, :LEAD].bitcast(I32), 0)
+        nc.vector.memset(g_scales[:, :LEAD].bitcast(I32), 0)
+        zeros = tile("zeros", [P, P], F32)
+        nc.vector.memset(zeros[:], 0.0)
 
-        x_woven0 = tile("x_woven0", [P, PACK, P, PACK], BF16)
-        nc.scalar.copy(*deal_views(x_woven0[:], x_raw[0][:], 0, PACK, slice(0, P)))
+        def deal(g):
+            woven = [tile(f"x{g}{u}_woven", [P, 2, P, PACK], BF16) for u in range(2)]
+            nc.vector.tensor_copy(*deal_views(woven[0][:], x_raw[g][:], 0, 2))
+            nc.scalar.copy(*deal_views(woven[1][:], x_raw[g][:], 2, 2))
+            return woven
 
-        v_pairs = tile("v_pairs", [P, N], U32)
-        nc.vector.tensor_copy(v_pairs[:], v_raw[:].indirect(offsets[:]))
-        v_codes = [tile(f"v_codes{o}", [P, 2 * N], U8) for o in range(PASSES)]
-        for o in range(PASSES):
-            nc.vector.tensor_copy(v_codes[o][:].bitcast(U16), v_pairs[:].bitcast(U16)[:, o::2])
+        def quantize_rows(g, woven):
+            return [quantize(f"x{g}{u}", woven[u][:].rearrange("p r s t -> p (r s t)"), 2 * P, E4M3) for u in range(2)]
 
-        hn = N // 2
-        halves = [slice(h * hn, (h + 1) * hn) for h in range(2)]
-        for t in range(PACK - 1):
-            nc.vector.tensor_copy(w_planes[1][:, t, :], w_raw[1][t][:].indirect(offsets[:]))
-            if t == 1:
-                nc.scalar.activation(*weave_views(w_woven[1][:, :, 0:2], w_planes[1][:, 0:2, :]), COPY, scale=-1.0)
-        x0 = (tile("x0_codes", [P, R], U32, tag="w_raw12"), tile("x0_scales", [P, R], U8))
-        for u in range(2):
-            cols = slice(2 * u * P, 2 * (u + 1) * P)
-            nc.vector.quantize_mx(x0[0][:, cols].bitcast(E4M3), x0[1][:, cols], x_woven0[:, 2 * u : 2 * u + 2].rearrange("p r s t -> p (r s t)"))
+        def quantize_w(g, tags):
+            return [quantize(f"w{g}{h}", w[g][h][:].rearrange("p n t -> p (n t)"), HALF, E4M3, tag=tags[h]) for h in range(2)]
+
+        w0 = quantize_w(0, (None, None))
+        x0 = quantize_rows(0, deal(0))
+        w1 = quantize_w(1, ("x00_woven", "x01_woven"))
+
+        v_pairs = [tile(f"v_pairs{h}", [P, HALF], U32) for h in range(2)]
+        v_codes = {}
+
+        def part(o, first, count, codes=None):
+            if codes is None:
+                codes = tile(f"v_codes{o}{first}", [P, count, 2 * P], U8)[:]
+            words = v_pairs[first // 2][:, first % 2 * P : (first % 2 + count) * P].bitcast(U16)
+            nc.vector.tensor_copy(codes.rearrange("p q b -> p (q b)").bitcast(U16), words[:, o::PASSES])
+            for q in range(count):
+                v_codes[o, first + q] = codes[:, q, :]
+
         for h in range(2):
-            nc.vector.tensor_copy(w_planes[1][:, 3, halves[h]], w_raw[1][3][:].indirect(offsets[:, h * hn // 16 : (h + 1) * hn // 16]))
-        nc.scalar.activation(*weave_views(w_woven[1][:, halves[0], 2:4], w_planes[1][:, 2:4, halves[0]]), COPY, scale=-1.0)
-        nc.vector.tensor_scalar_mul(*weave_views(w_woven[1][:, halves[1], 2:4], w_planes[1][:, 2:4, halves[1]]), -1.0)
-        w1 = (tile("w1_codes", [P, N], U32), tile("w1_scales", [P, N], U8))
-        for cols in halves:
-            nc.vector.quantize_mx(w1[0][:, cols].bitcast(E4M3), w1[1][:, cols], w_woven[1][:, cols, :].rearrange("p n t -> p (n t)"))
+            nc.vector.tensor_copy(v_pairs[h][:], v_raw[:].indirect(entries(halves[h])))
+            part(0, 2 * h, 2)
+        part(1, 0, 1)
 
-        scores = [ps.tile([P, N], F32, name=f"scores{r}") for r in range(PACK)]
+        scores = [ps.tile([P, PACK, P], F32, name=f"scores{q}", tag=f"scores{q}") for q in range(QUARTERS)]
 
-        def score_pass(r, x, cols, rhs, rhs_scale, start, stop):
+        def score_pass(q, r, x, cols, rhs, rhs_scale, start=False, stop=False):
             nc.tensor.matmul_mx(
-                scores[r][:],
+                scores[q][:, r, :],
                 lhsT=x[0][:, cols].bitcast(E4M3),
                 lhsT_scale=x[1][:, cols],
                 rhs=rhs,
@@ -142,82 +165,118 @@ def tile_attend_gds_sq_kernel(tc, xT, wT, v_words, v_scales, wt, xm, offs, out):
                 stop=stop,
             )
 
-        for r in range(PACK):
-            score_pass(r, x0, slice(r * P, (r + 1) * P), w0[0][:].bitcast(E4M3), w0[1][:], True, False)
-            score_pass(r, x0, slice(r * P, (r + 1) * P), v_codes[0][:].bitcast(E2M1), v_planes[:, 0, :], False, False)
+        def student(w, cols):
+            return w[0][:, cols].bitcast(E4M3), w[1][:, cols]
 
-        hp = P // 2
-        x1_view = x_raw[1][:].rearrange("p t (s r) -> p s t r", r=PACK)
-        x1 = []
-        for u in range(2):
-            codes, scales = tile(f"x1{u}_codes", [P, 2 * P], U32), tile(f"x1{u}_scales", [P, 2 * P], U8)
-            low = tile(f"x1{u}_low", [P, 2, hp, PACK], BF16, tag=("x10_low", "x10_high")[u])
-            high = tile(f"x1{u}_high", [P, 2, hp, PACK], BF16)
-            nc.vector.tensor_copy(low[:].rearrange("p r s t -> p s t r"), x1_view[:, 0:hp, :, 2 * u : 2 * u + 2])
-            nc.scalar.copy(high[:].rearrange("p r s t -> p s t r"), x1_view[:, hp:P, :, 2 * u : 2 * u + 2])
-            for r in range(2):
-                for h, woven in enumerate((low, high)):
-                    cols = slice(r * P + h * hp, r * P + (h + 1) * hp)
-                    nc.vector.quantize_mx(codes[:, cols].bitcast(E4M3), scales[:, cols], woven[:, r].rearrange("p s t -> p (s t)"))
-            x1.append((codes, scales))
+        def teacher(o, q):
+            return v_codes[o, q].bitcast(E2M1), v_planes[:, o, quarters[q]]
 
-        xm_q = []
+        for q in range(QUARTERS):
+            for r in range(PACK):
+                score_pass(q, r, x0[r // 2], quarters[r % 2], *student(w0[q // 2], quarters[q % 2]), start=r == 0)
+        for q in range(QUARTERS):
+            for r in range(PACK):
+                score_pass(q, r, x0[r // 2], quarters[r % 2], *teacher(0, q))
 
-        def xm_prepare(c, copy, tag):
+        x1_woven = deal(1)
+        x1 = [quantize(f"x1r{r}", x1_woven[r // 2][:, r % 2].rearrange("p s t -> p (s t)"), P, E4M3) for r in range(PACK)]
+
+        xm_woven, xm_q = [], []
+
+        def xm_weave(c, tag=None):
+            xm_woven.append(tile(f"xm_woven{c}", [P, XM_WIDTHS[c], PACK], BF16, tag=tag))
+            nc.scalar.copy(*weave_views(xm_woven[c][:], xm_raw[c][:]))
+
+        def xm_quantize(c, tag=None):
             width = XM_WIDTHS[c]
-            woven = tile(f"xm_woven{c}", [P, width, PACK], BF16, tag=tag)
-            copy(*weave_views(woven[:], xm_raw[c][:]))
-            codes, scales = quantize(f"xm{c}", woven[:].rearrange("p d t -> p (d t)"), width, E4M3)
-            xm_q.extend((c, codes[:, m : m + P], scales[:, m : m + P]) for m in range(0, width, P))
+            codes, scales = quantize(f"xm{c}", xm_woven[c][:].rearrange("p d t -> p (d t)"), width, E4M3, tag=tag)
+            xm_q.extend((codes[:, m : m + P], scales[:, m : m + P]) for m in range(0, width, P))
 
-        xm_prepare(0, nc.vector.tensor_copy, "x11_high")
+        g_woven = [tile(f"g_woven{q}", [P, P, PACK], BF16, tag=f"g_woven{q % 3}") for q in range(QUARTERS)]
+        wt_rows = wt_sb[:].unsqueeze(1).to_broadcast([P, P, PACK])
 
-        g_planes = [tile(f"g_planes{u}", [P, 2, N], BF16) for u in range(2)]
-        g_woven = tile("g_woven", [P, N, PACK], BF16)
-        for r in range(PACK):
-            cols = slice(r % 2 * P, (r % 2 + 1) * P)
-            score_pass(r, x1[r // 2], cols, v_codes[1][:].bitcast(E2M1), v_planes[:, 1, :], False, False)
-            score_pass(r, x1[r // 2], cols, w1[0][:].bitcast(E4M3), w1[1][:], False, True)
-            for cols in halves if r == PACK - 1 else [slice(0, N)]:
-                nc.scalar.activation(g_planes[r // 2][:, r % 2, cols], scores[r][:, cols], COPY, scale=wt_sb[:, r : r + 1])
-            if r == 1:
-                for cols in halves:
-                    nc.vector.tensor_copy(g_woven[:, cols, 0:2], g_planes[0][:, :, cols].rearrange("p t n -> p n t"))
+        def close_scores(q):
+            def student_pass(r):
+                score_pass(q, r, x1[r], quarters[0], *student(w1[q // 2], quarters[q % 2]), stop=q == 3 and r == PACK - 1)
+
+            def teacher_pass(r):
+                score_pass(q, r, x1[r], quarters[0], *teacher(1, q), stop=q < 3 and r == PACK - 1)
+
+            if q == 0:
+                for r in range(PACK):
+                    student_pass(r)
+                    teacher_pass(r)
+            else:
+                for kind in (student_pass, teacher_pass) if q < 3 else (teacher_pass, student_pass):
+                    for r in range(PACK):
+                        kind(r)
+
+        def weigh(q):
+            nc.vector.tensor_tensor(g_woven[q][:], scores[q][:].rearrange("p r n -> p n r"), wt_rows, MULT)
+
+        def quantize_g(q):
+            cols = slice(LEAD + q * P, LEAD + (q + 1) * P)
+            nc.vector.quantize_mx(g_codes[:, cols].bitcast(E5M2), g_scales[:, cols], g_woven[q][:].rearrange("p n t -> p (n t)"))
 
         grads = [ps.tile([P, N], F32, name=f"grad{b}") for b in range(4)]
+        g_planes = tile("g_planes", [P, PACK, P], BF16)
         dws = [tile(f"dw{j}", [P, N], F32) for j in range(D // P)]
 
-        def finish_g(cols):
-            nc.vector.tensor_copy(g_woven[:, cols, 2:4], g_planes[1][:, :, cols].rearrange("p t n -> p n t"))
-            nc.vector.quantize_mx(g_codes[:, cols].bitcast(E5M2), g_scales[:, cols], g_woven[:, cols, :].rearrange("p n t -> p (n t)"))
-
-        def gradient(j, bank, slots):
-            c, codes, scales = xm_q[j]
+        def gradient(j, bank, cols):
+            codes, scales = xm_q[j]
             nc.tensor.matmul_mx(
                 bank[:],
                 lhsT=codes.bitcast(E4M3),
                 lhsT_scale=scales,
-                rhs=g_codes[:].bitcast(E5M2),
-                rhs_scale=g_scales[:],
+                rhs=g_codes[:, cols].bitcast(E5M2),
+                rhs_scale=g_scales[:, cols],
                 start=True,
                 stop=True,
             )
-            nc.scalar.activation(dws[j][:, slots], bank[:, slots], COPY, scale=-1.0)
 
-        def scatter(j, slots):
-            entries = offsets[:, slots.start // 16 : slots.stop // 16]
-            nc.vector.tensor_copy(windows[j % WINDOWS][:].indirect(entries), dws[j][:, slots])
+        def scatter(j, slots, window):
+            nc.vector.tensor_copy(window[:].indirect(entries(slots)), dws[j][:, slots])
 
-        finish_g(halves[0])
-        gradient(0, grads[3], halves[0])
-        finish_g(halves[1])
-        xm_prepare(1, nc.scalar.copy, "after_g")
-        scatter(0, halves[0])
+        def store(j, window):
+            nc.sync.dma_start(out=out[j * P : (j + 1) * P, :], in_=window[:])
+
+        def empty(j, bank, slots, cols):
+            nc.scalar.activation(dws[j][:, slots], bank[:, cols], COPY, scale=-1.0)
+
+        for c in range(2):
+            xm_weave(c)
+        v_late = tile("v_late", [P, 2, 2 * P], U8, tag="x11_woven")
+        part(1, 1, 1, v_late[:, 0:1])
+        part(1, 2, 1, v_late[:, 1:2])
+        xm_quantize(0)
+        part(1, 3, 1, tile("v_last", [P, 1, 2 * P], U8, tag="v_pairs0")[:])
+        for q in range(QUARTERS):
+            close_scores(q)
+        weigh(0)
+        for r in range(PACK):
+            nc.scalar.activation(g_planes[:, r, :], scores[1][:, r, :], COPY, scale=wt_sb[:, r : r + 1])
+        nc.scalar.copy(*weave_views(g_woven[1][:], g_planes[:]))
+        weigh(2)
+        quantize_g(0)
+        xm_quantize(1)
+        for j in range(EARLY):
+            gradient(j, grads[j], slice(0, N))
+            empty(j, grads[j], quarters[0], slice(LEAD, N))
+        quantize_g(2)
+        weigh(3)
+        quantize_g(1)
+        quantize_g(3)
+        for j in range(EARLY):
+            nc.vector.tensor_tensor(windows[j][:].indirect(entries(quarters[0])), dws[j][:, quarters[0]], zeros[:], ADD)
+        xm_weave(2, tag="g_woven1")
+        xm_quantize(2)
         for j in range(D // P):
-            slots = halves[1] if j == 0 else slice(0, N)
-            gradient(j, grads[j % 4], slots)
-            scatter(j, slots)
-            nc.sync.dma_start(out=out[j * P : (j + 1) * P, :], in_=windows[j % WINDOWS][:])
-            c = xm_q[j][0]
-            if c + 2 < len(XM_WIDTHS) and xm_q[j + 1][0] != c:
-                xm_prepare(c + 2, nc.scalar.copy, f"xm{c}_codes")
+            slots = slice(P, N) if j < EARLY else slice(0, N)
+            bank = grads[(j + EARLY) % 4]
+            if j in (1, 2):
+                xm_weave(j + 2, tag=f"xm{j - 1}_codes")
+                xm_quantize(j + 2)
+            gradient(j, bank, slice(LEAD, LEAD + N))
+            empty(j, bank, slots, slots)
+            scatter(j, slots, windows[j % WINDOWS])
+            store(j, windows[j % WINDOWS])

@@ -16,17 +16,16 @@ E5M2 = mybir.dt.float8_e5m2_x4
 E2M1 = mybir.dt.float4_e2m1fn_x4
 COPY = mybir.ActivationFunctionType.Copy
 MULT = mybir.AluOpType.mult
-ADD = mybir.AluOpType.add
 
 P = 128
 PACK = 4
 K_PASS = P * PACK
 PASSES = D // K_PASS
-WINDOWS = 3
+TILES = D // P
+WINDOWS = 5
 QUARTERS = N // P
 HALF = N // 2
-LEAD = N - P
-EARLY = 2
+LEAD = HALF - 16
 XM_WIDTHS = (128, 128, 128, 128, 512)
 
 
@@ -53,7 +52,7 @@ def tile_attend_gds_sq_kernel(tc, xT, wT, v_words, v_scales, wt, xm, offs, out):
 
         w_raw = [[tile(f"w_raw{g}{t}", [P, T], F32) for t in range(PACK)] for g in range(PASSES)]
         w_rows = [wT[g * K_PASS : (g + 1) * K_PASS, :].rearrange("(p t) c -> p t c", t=PACK) for g in range(PASSES)]
-        x_raw = [tile(f"x_raw{g}", [P, PACK, R], F32) for g in range(PASSES)]
+        x_raw = [tile("x_raw0", [P, PACK, R], F32)]
         x_rows = [xT[0, g * K_PASS : (g + 1) * K_PASS, :].rearrange("(p t) r -> p t r", t=PACK) for g in range(PASSES)]
         wt_sb = tile("wt_sb", [P, PACK], F32)
         v_raw = tile("v_raw", [P, T], U32)
@@ -66,8 +65,14 @@ def tile_attend_gds_sq_kernel(tc, xT, wT, v_words, v_scales, wt, xm, offs, out):
         for t in range(PACK):
             nc.sync.dma_start(out=w_raw[1][t][:], in_=w_rows[1][:, t, :])
         nc.sync.dma_start(out=x_raw[0][:], in_=x_rows[0])
-        nc.sync.dma_start(out=v_raw[:].bitcast(I32), in_=v_words[0].rearrange("p t b -> p (t b)").bitcast(I32))
+        v_picked = tile("v_picked", [P, PASSES, N], U8)
+        for o in range(PASSES):
+            nc.vector.tensor_copy(v_picked[:, o, :], v_bytes[:, o, :].indirect(offsets[:]))
+        for q in range(0, P, 32):
+            nc.sync.dma_start(out=v_planes[q : q + 4, :, :].bitcast(I32), in_=v_picked[q : q + 32 : 8, :, :].bitcast(I32))
+        x_raw.append(tile("x_raw1", [P, PACK, R], F32, tag="v_bytes"))
         nc.sync.dma_start(out=x_raw[1][:], in_=x_rows[1])
+        nc.sync.dma_start(out=v_raw[:].bitcast(I32), in_=v_words[0].rearrange("p t b -> p (t b)").bitcast(I32))
         nc.sync.dma_start(out=wt_sb[:], in_=wt[0].rearrange("(p t) o -> p (t o)", t=PACK))
         xm_rows = xm[0].rearrange("(p t) d -> p t d", t=PACK)
         xm_raw = []
@@ -94,31 +99,21 @@ def tile_attend_gds_sq_kernel(tc, xT, wT, v_words, v_scales, wt, xm, offs, out):
             nc.vector.quantize_mx(codes[:].bitcast(fmt), scales[:], woven)
             return codes, scales
 
-        v_picked = tile("v_picked", [P, PASSES, N], U8)
-        for o in range(PASSES):
-            nc.vector.tensor_copy(v_picked[:, o, :], v_bytes[:, o, :].indirect(offsets[:]))
-        for q in range(0, P, 32):
-            nc.scalar.dma_start(out=v_planes[q : q + 4, :, :].bitcast(I32), in_=v_picked[q : q + 32 : 8, :, :].bitcast(I32))
-
         w = []
         windows = [tile(f"window{j}", [P, T], F32) for j in range(WINDOWS)]
         for g in range(PASSES):
             planes = tile(f"w_planes{g}", [P, PACK, N], BF16)
             woven = [tile(f"w_woven{g}{h}", [P, HALF, PACK], BF16) for h in range(2)]
             for t in range(PACK):
-                nc.vector.tensor_copy(planes[:, t, :], w_raw[g][t][:].indirect(offsets[:]))
-                if g == 0 and t > 0:
-                    nc.vector.memset(windows[t - 1][:].bitcast(I32), 0)
+                if g == PASSES - 1 and t == PACK - 1:
+                    nc.vector.tensor_copy(planes[:, t, :], w_raw[g][t][:].indirect(offsets[:]))
+                else:
+                    nc.scalar.activation(planes[:, t, :], w_raw[g][t][:].indirect(offsets[:]), COPY)
+                if 0 < g * PACK + t <= WINDOWS:
+                    nc.vector.memset(windows[g * PACK + t - 1][:].bitcast(I32), 0)
             nc.scalar.activation(*weave_views(woven[0][:], planes[:, :, halves[0]]), COPY, scale=-1.0)
             nc.vector.tensor_scalar_mul(*weave_views(woven[1][:], planes[:, :, halves[1]]), -1.0)
             w.append(woven)
-
-        g_codes = tile("g_codes", [P, LEAD + N], U32)
-        g_scales = tile("g_scales", [P, LEAD + N], U8)
-        nc.vector.memset(g_codes[:, :LEAD].bitcast(I32), 0)
-        nc.vector.memset(g_scales[:, :LEAD].bitcast(I32), 0)
-        zeros = tile("zeros", [P, P], F32)
-        nc.vector.memset(zeros[:], 0.0)
 
         def deal(g):
             woven = [tile(f"x{g}{u}_woven", [P, 2, P, PACK], BF16) for u in range(2)]
@@ -126,157 +121,182 @@ def tile_attend_gds_sq_kernel(tc, xT, wT, v_words, v_scales, wt, xm, offs, out):
             nc.scalar.copy(*deal_views(woven[1][:], x_raw[g][:], 2, 2))
             return woven
 
-        def quantize_rows(g, woven):
-            return [quantize(f"x{g}{u}", woven[u][:].rearrange("p r s t -> p (r s t)"), 2 * P, E4M3) for u in range(2)]
-
         def quantize_w(g, tags):
             return [quantize(f"w{g}{h}", w[g][h][:].rearrange("p n t -> p (n t)"), HALF, E4M3, tag=tags[h]) for h in range(2)]
 
-        w0 = quantize_w(0, (None, None))
-        x0 = quantize_rows(0, deal(0))
-        w1 = quantize_w(1, ("x00_woven", "x01_woven"))
-
-        v_pairs = [tile(f"v_pairs{h}", [P, HALF], U32) for h in range(2)]
-        v_codes = {}
-
-        def part(o, first, count, codes=None):
-            if codes is None:
-                codes = tile(f"v_codes{o}{first}", [P, count, 2 * P], U8)[:]
-            words = v_pairs[first // 2][:, first % 2 * P : (first % 2 + count) * P].bitcast(U16)
-            nc.vector.tensor_copy(codes.rearrange("p q b -> p (q b)").bitcast(U16), words[:, o::PASSES])
-            for q in range(count):
-                v_codes[o, first + q] = codes[:, q, :]
-
-        for h in range(2):
-            nc.vector.tensor_copy(v_pairs[h][:], v_raw[:].indirect(entries(halves[h])))
-            part(0, 2 * h, 2)
-        part(1, 0, 1)
+        def quantize_rows(g, woven):
+            return [quantize(f"x{g}{u}", woven[u][:].rearrange("p r s t -> p (r s t)"), 2 * P, E4M3) for u in range(2)]
 
         scores = [ps.tile([P, PACK, P], F32, name=f"scores{q}", tag=f"scores{q}") for q in range(QUARTERS)]
 
-        def score_pass(q, r, x, cols, rhs, rhs_scale, start=False, stop=False):
+        def score_pass(q, r, x, rhs, rhs_scale, start=False, stop=False):
+            codes, scales = x[r // 2]
             nc.tensor.matmul_mx(
                 scores[q][:, r, :],
-                lhsT=x[0][:, cols].bitcast(E4M3),
-                lhsT_scale=x[1][:, cols],
+                lhsT=codes[:, quarters[r % 2]].bitcast(E4M3),
+                lhsT_scale=scales[:, quarters[r % 2]],
                 rhs=rhs,
                 rhs_scale=rhs_scale,
                 start=start,
                 stop=stop,
             )
 
-        def student(w, cols):
-            return w[0][:, cols].bitcast(E4M3), w[1][:, cols]
+        x = []
+        for g in range(PASSES):
+            w_q = quantize_w(g, ("x00_woven", "x01_woven") if g else (None, None))
+            x.append(quantize_rows(g, deal(g)))
+            for q in range(QUARTERS):
+                codes, scales = w_q[q // 2]
+                for r in range(PACK):
+                    score_pass(q, r, x[g], codes[:, quarters[q % 2]].bitcast(E4M3), scales[:, quarters[q % 2]], start=g == 0 and r == 0)
 
-        def teacher(o, q):
-            return v_codes[o, q].bitcast(E2M1), v_planes[:, o, quarters[q]]
+        v_pairs = {}
 
-        for q in range(QUARTERS):
-            for r in range(PACK):
-                score_pass(q, r, x0[r // 2], quarters[r % 2], *student(w0[q // 2], quarters[q % 2]), start=r == 0)
-        for q in range(QUARTERS):
-            for r in range(PACK):
-                score_pass(q, r, x0[r // 2], quarters[r % 2], *teacher(0, q))
+        def gather_words(first, count):
+            pairs = tile(f"v_pairs{first}", [P, count * P], U32, tag=f"v_pairs{first % 2}")
+            nc.vector.tensor_copy(pairs[:], v_raw[:].indirect(entries(slice(first * P, (first + count) * P))))
+            for q in range(count):
+                v_pairs[first + q] = pairs[:, q * P : (q + 1) * P]
 
-        x1_woven = deal(1)
-        x1 = [quantize(f"x1r{r}", x1_woven[r // 2][:, r % 2].rearrange("p s t -> p (s t)"), P, E4M3) for r in range(PACK)]
+        v_codes = {}
 
-        xm_woven, xm_q = [], []
-
-        def xm_weave(c, tag=None):
-            xm_woven.append(tile(f"xm_woven{c}", [P, XM_WIDTHS[c], PACK], BF16, tag=tag))
-            nc.scalar.copy(*weave_views(xm_woven[c][:], xm_raw[c][:]))
-
-        def xm_quantize(c, tag=None):
-            width = XM_WIDTHS[c]
-            codes, scales = quantize(f"xm{c}", xm_woven[c][:].rearrange("p d t -> p (d t)"), width, E4M3, tag=tag)
-            xm_q.extend((codes[:, m : m + P], scales[:, m : m + P]) for m in range(0, width, P))
-
-        g_woven = [tile(f"g_woven{q}", [P, P, PACK], BF16, tag=f"g_woven{q % 3}") for q in range(QUARTERS)]
-        wt_rows = wt_sb[:].unsqueeze(1).to_broadcast([P, P, PACK])
+        def part_words(q):
+            codes = tile(f"v_codes{q}", [P, PASSES, 2 * P], U8)
+            nc.vector.tensor_copy(
+                codes[:].rearrange("p o b -> p (o b)").bitcast(U16).rearrange("p (o n) -> p o n", o=PASSES),
+                v_pairs[q].bitcast(U16).rearrange("p (n o) -> p o n", o=PASSES),
+            )
+            v_codes[q] = codes
 
         def close_scores(q):
-            def student_pass(r):
-                score_pass(q, r, x1[r], quarters[0], *student(w1[q // 2], quarters[q % 2]), stop=q == 3 and r == PACK - 1)
-
-            def teacher_pass(r):
-                score_pass(q, r, x1[r], quarters[0], *teacher(1, q), stop=q < 3 and r == PACK - 1)
-
-            if q == 0:
+            for o in range(PASSES):
                 for r in range(PACK):
-                    student_pass(r)
-                    teacher_pass(r)
-            else:
-                for kind in (student_pass, teacher_pass) if q < 3 else (teacher_pass, student_pass):
-                    for r in range(PACK):
-                        kind(r)
+                    score_pass(q, r, x[o], v_codes[q][:, o, :].bitcast(E2M1), v_planes[:, o, quarters[q]], stop=o == PASSES - 1 and r == PACK - 1)
+
+        xm_woven, xm_q = {}, {}
+        xm_cols = [raw[:, :, m : m + P] for raw, width in zip(xm_raw, XM_WIDTHS) for m in range(0, width, P)]
+
+        def xm_weave(c, copy, tag=None):
+            xm_woven[c] = tile(f"xm_woven{c}", [P, P, PACK], BF16, tag=tag)
+            copy(*weave_views(xm_woven[c][:], xm_cols[c]))
+
+        def xm_quantize(c, tag=None):
+            codes, scales = quantize(f"xm{c}", xm_woven[c][:].rearrange("p d t -> p (d t)"), P, E4M3, tag=tag)
+            xm_q[c] = codes[:], scales[:]
+
+        g_woven = [tile(f"g_woven{q}", [P, P, PACK], BF16, tag=f"g_woven{q % 2}") for q in range(QUARTERS)]
+        g_codes = tile("g_codes", [P, N], U32)
+        g_scales = tile("g_scales", [P, N], U8)
+        wt_rows = wt_sb[:].unsqueeze(1).to_broadcast([P, P, PACK])
 
         def weigh(q):
             nc.vector.tensor_tensor(g_woven[q][:], scores[q][:].rearrange("p r n -> p n r"), wt_rows, MULT)
 
         def quantize_g(q):
-            cols = slice(LEAD + q * P, LEAD + (q + 1) * P)
-            nc.vector.quantize_mx(g_codes[:, cols].bitcast(E5M2), g_scales[:, cols], g_woven[q][:].rearrange("p n t -> p (n t)"))
+            nc.vector.quantize_mx(
+                g_codes[:, quarters[q]].bitcast(E5M2), g_scales[:, quarters[q]], g_woven[q][:].rearrange("p n t -> p (n t)")
+            )
 
-        grads = [ps.tile([P, N], F32, name=f"grad{b}") for b in range(4)]
-        g_planes = tile("g_planes", [P, PACK, P], BF16)
-        dws = [tile(f"dw{j}", [P, N], F32) for j in range(D // P)]
+        dws = {}
 
-        def gradient(j, bank, cols):
+        def bank_tile(name, tag):
+            return ps.tile([P, N], F32, name=name, tag=tag)
+
+        def gradient(j, slots, target):
             codes, scales = xm_q[j]
             nc.tensor.matmul_mx(
-                bank[:],
+                target,
                 lhsT=codes.bitcast(E4M3),
                 lhsT_scale=scales,
-                rhs=g_codes[:, cols].bitcast(E5M2),
-                rhs_scale=g_scales[:, cols],
+                rhs=g_codes[:, slots].bitcast(E5M2),
+                rhs_scale=g_scales[:, slots],
                 start=True,
                 stop=True,
             )
+            return target
 
-        def scatter(j, slots, window):
-            nc.vector.tensor_copy(window[:].indirect(entries(slots)), dws[j][:, slots])
+        def empty_scalar(j, h, source):
+            dws[j, h] = tile(f"dw{j}{h}", [P, HALF], F32)[:]
+            nc.scalar.activation(dws[j, h], source, COPY, scale=-1.0)
 
-        def store(j, window):
-            nc.sync.dma_start(out=out[j * P : (j + 1) * P, :], in_=window[:])
+        def empty_vector(j, h, source):
+            dws[j, h] = tile(f"dw{j}{h}", [P, HALF], F32)[:]
+            nc.vector.tensor_scalar_mul(dws[j, h], source, -1.0)
 
-        def empty(j, bank, slots, cols):
-            nc.scalar.activation(dws[j][:, slots], bank[:, cols], COPY, scale=-1.0)
+        def window(j, h):
+            return windows[j % WINDOWS][:].indirect(entries(halves[h]))
 
-        for c in range(2):
-            xm_weave(c)
-        v_late = tile("v_late", [P, 2, 2 * P], U8, tag="x11_woven")
-        part(1, 1, 1, v_late[:, 0:1])
-        part(1, 2, 1, v_late[:, 1:2])
-        xm_quantize(0)
-        part(1, 3, 1, tile("v_last", [P, 1, 2 * P], U8, tag="v_pairs0")[:])
-        for q in range(QUARTERS):
+        def scatter_scalar(j, h):
+            nc.scalar.activation(window(j, h), dws[j, h], COPY)
+
+        def scatter_vector(j, h):
+            nc.vector.tensor_copy(window(j, h), dws[j, h])
+
+        def store(j):
+            nc.sync.dma_start(out=out[j * P : (j + 1) * P, :], in_=windows[j % WINDOWS][:])
+
+        tags = [f"grad{b}" for b in range(4)] + [f"scores{q}" for q in range(QUARTERS)]
+        first, shared = (bank_tile(f"early{b}", tags[b]) for b in range(2))
+
+        def half(j, h):
+            bank = bank_tile(f"half{j}{h}", tags[2 * j + h - 1])
+            (empty_scalar if h else empty_vector)(j, h, gradient(j, halves[h], bank[:, halves[0]]))
+
+        def whole(j):
+            bank = bank_tile(f"whole{j}", tags[(j + 3) % len(tags)])
+            gradient(j, slice(0, N), bank[:])
+            for h in range(2):
+                empty_scalar(j, h, bank[:, halves[h]])
+
+        gather_words(0, 1)
+        gather_words(1, 1)
+        for q in range(2):
+            part_words(q)
             close_scores(q)
-        weigh(0)
-        for r in range(PACK):
-            nc.scalar.activation(g_planes[:, r, :], scores[1][:, r, :], COPY, scale=wt_sb[:, r : r + 1])
-        nc.scalar.copy(*weave_views(g_woven[1][:], g_planes[:]))
-        weigh(2)
-        quantize_g(0)
+        gather_words(2, 2)
+        for c in range(4):
+            xm_weave(c, nc.scalar.copy)
+        xm_quantize(0)
+        for q in range(2, QUARTERS):
+            part_words(q)
+        for q in range(2):
+            weigh(q)
+        for q in range(2):
+            quantize_g(q)
+        empty_scalar(0, 0, gradient(0, halves[0], first[:, halves[0]]))
+        scatter_scalar(0, 0)
+        for q in range(2, QUARTERS):
+            close_scores(q)
         xm_quantize(1)
-        for j in range(EARLY):
-            gradient(j, grads[j], slice(0, N))
-            empty(j, grads[j], quarters[0], slice(LEAD, N))
-        quantize_g(2)
+        gradient(1, halves[0], shared[:, halves[0]])
+        pair = tile("dw_pair", [P, N], F32)
+        dws[1, 0], dws[0, 1] = pair[:, halves[0]], pair[:, halves[1]]
+        weigh(2)
+        nc.vector.tensor_scalar_mul(pair[:, :LEAD], shared[:, :LEAD], -1.0)
         weigh(3)
-        quantize_g(1)
-        quantize_g(3)
-        for j in range(EARLY):
-            nc.vector.tensor_tensor(windows[j][:].indirect(entries(quarters[0])), dws[j][:, quarters[0]], zeros[:], ADD)
-        xm_weave(2, tag="g_woven1")
+        for q in range(2, QUARTERS):
+            quantize_g(q)
+        gradient(0, halves[1], shared[:, halves[1]])
         xm_quantize(2)
-        for j in range(D // P):
-            slots = slice(P, N) if j < EARLY else slice(0, N)
-            bank = grads[(j + EARLY) % 4]
-            if j in (1, 2):
-                xm_weave(j + 2, tag=f"xm{j - 1}_codes")
+        xm_quantize(3)
+        xm_weave(4, nc.vector.tensor_copy)
+        nc.vector.tensor_scalar_mul(pair[:, LEAD:], shared[:, LEAD:], -1.0)
+        half(1, 1)
+        scatter_scalar(0, 1)
+        store(0)
+        holds = {5: "xm_woven4", 6: "dw30", 7: "dw40"}
+        for j in range(1, TILES):
+            scatter_vector(j, 0)
+            if 3 <= j <= 5:
                 xm_quantize(j + 2)
-            gradient(j, bank, slice(LEAD, LEAD + N))
-            empty(j, bank, slots, slots)
-            scatter(j, slots, windows[j % WINDOWS])
-            store(j, windows[j % WINDOWS])
+            if j <= 2:
+                for h in range(2):
+                    half(j + 1, h)
+            elif j + 1 < TILES:
+                whole(j + 1)
+            if j == 1:
+                xm_quantize(4)
+            if 2 <= j <= 4:
+                xm_weave(j + 3, nc.vector.tensor_copy, tag=holds[j + 3])
+            scatter_scalar(j, 1)
+            store(j)

@@ -25,8 +25,7 @@ TILES = D // P
 WINDOWS = 5
 QUARTERS = N // P
 HALF = N // 2
-LEAD = HALF - 16
-XM_WIDTHS = (128, 128, 128, 128, 512)
+XM_WIDTHS = (256, 128, 128, 128, 384)
 
 
 def tile_attend_gds_sq_kernel(tc, xT, wT, v_words, v_scales, wt, xm, offs, out):
@@ -161,7 +160,7 @@ def tile_attend_gds_sq_kernel(tc, xT, wT, v_words, v_scales, wt, xm, offs, out):
         v_codes = {}
 
         def part_words(q):
-            codes = tile(f"v_codes{q}", [P, PASSES, 2 * P], U8)
+            codes = tile(f"v_codes{q}", [P, PASSES, 2 * P], U8, tag=f"v_codes{q % 3}")
             nc.vector.tensor_copy(
                 codes[:].rearrange("p o b -> p (o b)").bitcast(U16).rearrange("p (o n) -> p o n", o=PASSES),
                 v_pairs[q].bitcast(U16).rearrange("p (n o) -> p o n", o=PASSES),
@@ -245,8 +244,13 @@ def tile_attend_gds_sq_kernel(tc, xT, wT, v_words, v_scales, wt, xm, offs, out):
         def whole(j):
             bank = bank_tile(f"whole{j}", tags[(j + 3) % len(tags)])
             gradient(j, slice(0, N), bank[:])
-            for h in range(2):
-                empty_scalar(j, h, bank[:, halves[h]])
+            if j == WINDOWS:
+                for h in range(2):
+                    empty_scalar(j, h, bank[:, halves[h]])
+            else:
+                dw = tile(f"dw{j}", [P, N], F32, tag=f"dw{WINDOWS}0" if j == TILES - 1 else None)
+                nc.scalar.activation(dw[:], bank[:], COPY, scale=-1.0)
+                dws[j, 0], dws[j, 1] = dw[:, halves[0]], dw[:, halves[1]]
 
         gather_words(0, 1)
         gather_words(1, 1)
@@ -256,35 +260,34 @@ def tile_attend_gds_sq_kernel(tc, xT, wT, v_words, v_scales, wt, xm, offs, out):
         gather_words(2, 2)
         for c in range(4):
             xm_weave(c, nc.scalar.copy)
-        xm_quantize(0)
-        for q in range(2, QUARTERS):
-            part_words(q)
-        for q in range(2):
-            weigh(q)
-        for q in range(2):
+        part_words(2)
+        weigh(0)
+        part_words(3)
+        weigh(1)
+        xm_quantize(0, tag="v_pairs0")
+        dws[0, 0] = tile("dw00", [P, HALF], F32)[:]
+        for q, bank in enumerate((first, bank_tile("early_second", "scores0"))):
             quantize_g(q)
-        empty_scalar(0, 0, gradient(0, halves[0], first[:, halves[0]]))
+            nc.scalar.activation(dws[0, 0][:, quarters[q]], gradient(0, quarters[q], bank[:, quarters[0]]), COPY, scale=-1.0)
         scatter_scalar(0, 0)
         for q in range(2, QUARTERS):
             close_scores(q)
-        xm_quantize(1)
+        xm_quantize(1, tag="v_codes1")
         gradient(1, halves[0], shared[:, halves[0]])
-        pair = tile("dw_pair", [P, N], F32)
-        dws[1, 0], dws[0, 1] = pair[:, halves[0]], pair[:, halves[1]]
-        weigh(2)
-        nc.vector.tensor_scalar_mul(pair[:, :LEAD], shared[:, :LEAD], -1.0)
-        weigh(3)
+        for q in range(2, QUARTERS):
+            weigh(q)
         for q in range(2, QUARTERS):
             quantize_g(q)
         gradient(0, halves[1], shared[:, halves[1]])
-        xm_quantize(2)
-        xm_quantize(3)
-        xm_weave(4, nc.vector.tensor_copy)
-        nc.vector.tensor_scalar_mul(pair[:, LEAD:], shared[:, LEAD:], -1.0)
+        xm_quantize(2, tag="v_codes0")
+        xm_quantize(3, tag="g_woven0")
+        xm_weave(4, nc.vector.tensor_copy, tag="g_woven1")
+        empty_vector(0, 1, shared[:, halves[1]])
+        empty_vector(1, 0, shared[:, halves[0]])
         half(1, 1)
         scatter_scalar(0, 1)
         store(0)
-        holds = {5: "xm_woven4", 6: "dw30", 7: "dw40"}
+        holds = {5: "g_woven1", 6: "dw20", 7: "dw30"}
         for j in range(1, TILES):
             scatter_vector(j, 0)
             if 3 <= j <= 5:

@@ -49,20 +49,24 @@ def tile_attend_gds_sq_kernel(tc, xT, wT, v_words, v_scales, wt, xm, offs, out):
         v_planes = tile("v_planes", [P, PASSES, N], U8)
         nc.vector.memset(v_planes[:].rearrange("p o t -> p (o t)").bitcast(I32), 0)
 
-        w_raw = [[tile(f"w_raw{g}{t}", [P, T], F32) for t in range(PACK)] for g in range(PASSES)]
+        w_first, w_last = tile("w_first", [P, T], F32), tile("w_last", [P, T], F32)
+        w_three = [tile(f"w_three{g}", [P, PACK - 1, T], F32) for g in range(PASSES)]
+        w_raw = [
+            [w_first[:]] + [w_three[0][:, t, :] for t in range(PACK - 1)],
+            [w_three[1][:, t, :] for t in range(PACK - 1)] + [w_last[:]],
+        ]
         w_rows = [wT[g * K_PASS : (g + 1) * K_PASS, :].rearrange("(p t) c -> p t c", t=PACK) for g in range(PASSES)]
         x_raw = [tile("x_raw0", [P, PACK, R], F32)]
         x_rows = [xT[0, g * K_PASS : (g + 1) * K_PASS, :].rearrange("(p t) r -> p t r", t=PACK) for g in range(PASSES)]
         wt_sb = tile("wt_sb", [P, PACK], F32)
         v_raw = tile("v_raw", [P, T], U32)
 
-        nc.sync.dma_start(out=w_raw[0][0][:], in_=w_rows[0][:, 0, :])
+        nc.sync.dma_start(out=w_first[:], in_=w_rows[0][:, 0, :])
         nc.sync.dma_start(offsets[:], offs)
         nc.sync.dma_start(out=v_bytes[0:P:8, :, :].bitcast(I32), in_=v_scales.rearrange("o f t -> f o t").bitcast(I32))
-        for t in range(1, PACK):
-            nc.sync.dma_start(out=w_raw[0][t][:], in_=w_rows[0][:, t, :])
-        for t in range(PACK):
-            nc.sync.dma_start(out=w_raw[1][t][:], in_=w_rows[1][:, t, :])
+        nc.sync.dma_start(out=w_three[0][:], in_=w_rows[0][:, 1:, :])
+        nc.sync.dma_start(out=w_three[1][:], in_=w_rows[1][:, : PACK - 1, :])
+        nc.sync.dma_start(out=w_last[:], in_=w_rows[1][:, PACK - 1, :])
         nc.sync.dma_start(out=x_raw[0][:], in_=x_rows[0])
         v_picked = tile("v_picked", [P, PASSES, N], U8)
         for o in range(PASSES):
@@ -101,13 +105,13 @@ def tile_attend_gds_sq_kernel(tc, xT, wT, v_words, v_scales, wt, xm, offs, out):
         w = []
         windows = [tile(f"window{j}", [P, T], F32) for j in range(WINDOWS)]
         for g in range(PASSES):
-            planes = tile(f"w_planes{g}", [P, PACK, N], BF16)
+            planes = tile(f"w_planes{g}", [P, PACK, N], F32)
             woven = [tile(f"w_woven{g}{h}", [P, HALF, PACK], BF16) for h in range(2)]
             for t in range(PACK):
-                if g == PASSES - 1 and t == PACK - 1:
-                    nc.vector.tensor_copy(planes[:, t, :], w_raw[g][t][:].indirect(offsets[:]))
+                if g == PASSES - 1 and t in (0, PACK - 1):
+                    nc.vector.tensor_copy(planes[:, t, :], w_raw[g][t].indirect(offsets[:]))
                 else:
-                    nc.scalar.activation(planes[:, t, :], w_raw[g][t][:].indirect(offsets[:]), COPY)
+                    nc.scalar.activation(planes[:, t, :], w_raw[g][t].indirect(offsets[:]), COPY)
                 if 0 < g * PACK + t <= WINDOWS:
                     nc.vector.memset(windows[g * PACK + t - 1][:].bitcast(I32), 0)
             nc.scalar.activation(*weave_views(woven[0][:], planes[:, :, halves[0]]), COPY, scale=-1.0)

@@ -222,8 +222,8 @@ def tile_attend_gds_sq_kernel(tc, xT, wT, v_words, v_scales, wt, xm, offs, out):
             dws[j, h] = tile(f"dw{j}{h}", [P, HALF], F32)[:]
             nc.scalar.activation(dws[j, h], source, COPY, scale=-1.0)
 
-        def empty_vector(j, h, source):
-            dws[j, h] = tile(f"dw{j}{h}", [P, HALF], F32)[:]
+        def empty_vector(j, h, source, tag=None):
+            dws[j, h] = tile(f"dw{j}{h}", [P, HALF], F32, tag=tag)[:]
             nc.vector.tensor_scalar_mul(dws[j, h], source, -1.0)
 
         def window(j, h):
@@ -246,13 +246,13 @@ def tile_attend_gds_sq_kernel(tc, xT, wT, v_words, v_scales, wt, xm, offs, out):
             (empty_scalar if h else empty_vector)(j, h, gradient(j, halves[h], bank[:, halves[0]]))
 
         def whole(j):
-            bank = bank_tile(f"whole{j}", tags[(j + 3) % len(tags)])
+            bank = bank_tile(f"whole{j}", tags[3 if j == 4 else (j + 3) % len(tags)])
             gradient(j, slice(0, N), bank[:])
-            if j == WINDOWS:
+            if j == 5:
                 for h in range(2):
                     empty_scalar(j, h, bank[:, halves[h]])
             else:
-                dw = tile(f"dw{j}", [P, N], F32, tag=f"dw{WINDOWS}0" if j == TILES - 1 else None)
+                dw = tile(f"dw{j}", [P, N], F32, tag="dw50" if j == TILES - 1 else None)
                 nc.scalar.activation(dw[:], bank[:], COPY, scale=-1.0)
                 dws[j, 0], dws[j, 1] = dw[:, halves[0]], dw[:, halves[1]]
 
@@ -262,7 +262,7 @@ def tile_attend_gds_sq_kernel(tc, xT, wT, v_words, v_scales, wt, xm, offs, out):
             part_words(q)
             close_scores(q)
         gather_words(2, 2)
-        for c in range(4):
+        for c in range(5):
             xm_weave(c, nc.scalar.copy)
         part_words(2)
         weigh(0)
@@ -277,21 +277,21 @@ def tile_attend_gds_sq_kernel(tc, xT, wT, v_words, v_scales, wt, xm, offs, out):
         for q in range(2, QUARTERS):
             close_scores(q)
         xm_quantize(1, tag="v_codes1")
-        gradient(1, halves[0], shared[:, halves[0]])
+        second = gradient(1, halves[0], bank_tile("half10", "scores1")[:, halves[0]])
         for q in range(2, QUARTERS):
             weigh(q)
-        for q in range(2, QUARTERS):
-            quantize_g(q)
-        gradient(0, halves[1], shared[:, halves[1]])
+        dws[0, 1] = tile("dw01", [P, HALF], F32)[:]
+        for q, bank in enumerate((shared, bank_tile("early_last", "scores2"))):
+            quantize_g(2 + q)
+            nc.vector.tensor_scalar_mul(dws[0, 1][:, quarters[q]], gradient(0, quarters[2 + q], bank[:, quarters[0]]), -1.0)
+        empty_vector(1, 0, second, tag="g_woven0")
         xm_quantize(2, tag="v_codes0")
-        xm_quantize(3, tag="g_woven0")
-        xm_weave(4, nc.vector.tensor_copy, tag="g_woven1")
-        empty_vector(0, 1, shared[:, halves[1]])
-        empty_vector(1, 0, shared[:, halves[0]])
+        xm_quantize(3, tag="g_woven1")
+        xm_quantize(4, tag="xm_woven3")
         half(1, 1)
         scatter_scalar(0, 1)
         store(0)
-        holds = {5: "g_woven1", 6: "dw20", 7: "dw30"}
+        holds = {5: "g_woven0", 6: "dw20", 7: "dw30"}
         for j in range(1, TILES):
             scatter_vector(j, 0)
             if 3 <= j <= 5:
@@ -301,8 +301,6 @@ def tile_attend_gds_sq_kernel(tc, xT, wT, v_words, v_scales, wt, xm, offs, out):
                     half(j + 1, h)
             elif j + 1 < TILES:
                 whole(j + 1)
-            if j == 1:
-                xm_quantize(4)
             if 2 <= j <= 4:
                 xm_weave(j + 3, nc.vector.tensor_copy, tag=holds[j + 3])
             scatter_scalar(j, 1)

@@ -16,6 +16,7 @@ E5M2 = mybir.dt.float8_e5m2_x4
 E2M1 = mybir.dt.float4_e2m1fn_x4
 COPY = mybir.ActivationFunctionType.Copy
 MULT = mybir.AluOpType.mult
+ADD = mybir.AluOpType.add
 
 P = 128
 PACK = 4
@@ -183,6 +184,9 @@ def tile_attend_gds_sq_kernel(tc, xT, wT, v_words, v_scales, wt, xm, offs, out):
             xm_woven[c] = tile(f"xm_woven{c}", [P, P, PACK], BF16, tag=tag)
             copy(*weave_views(xm_woven[c][:], xm_cols[c]))
 
+        def weave_gpsimd(dst, src):
+            nc.gpsimd.tensor_scalar(dst, src, 1.0, 0.0, MULT, ADD)
+
         def xm_quantize(c, tag=None):
             codes, scales = quantize(f"xm{c}", xm_woven[c][:].rearrange("p d t -> p (d t)"), P, E4M3, tag=tag)
             xm_q[c] = codes[:], scales[:]
@@ -302,6 +306,6 @@ def tile_attend_gds_sq_kernel(tc, xT, wT, v_words, v_scales, wt, xm, offs, out):
             elif j + 1 < TILES:
                 whole(j + 1)
             if 2 <= j <= 4:
-                xm_weave(j + 3, nc.vector.tensor_copy, tag=holds[j + 3])
+                xm_weave(j + 3, weave_gpsimd, tag=holds[j + 3])
             scatter_scalar(j, 1)
             store(j)

@@ -252,11 +252,11 @@ def tile_attend_gds_sq_kernel(tc, xT, wT, v_words, v_scales, wt, xm, offs, out):
         def whole(j):
             bank = bank_tile(f"whole{j}", tags[3 if j == 4 else (j + 3) % len(tags)])
             gradient(j, slice(0, N), bank[:])
-            if j == 5:
-                for h in range(2):
-                    empty_scalar(j, h, bank[:, halves[h]])
+            if j % 2:
+                empty_vector(j, 0, bank[:, halves[0]], tag="dw30")
+                empty_scalar(j, 1, bank[:, halves[1]])
             else:
-                dw = tile(f"dw{j}", [P, N], F32, tag="dw50" if j == TILES - 1 else None)
+                dw = tile(f"dw{j}", [P, N], F32)
                 nc.scalar.activation(dw[:], bank[:], COPY, scale=-1.0)
                 dws[j, 0], dws[j, 1] = dw[:, halves[0]], dw[:, halves[1]]
 
@@ -295,7 +295,7 @@ def tile_attend_gds_sq_kernel(tc, xT, wT, v_words, v_scales, wt, xm, offs, out):
         half(1, 1)
         scatter_scalar(0, 1)
         store(0)
-        holds = {5: "g_woven0", 6: "dw20", 7: "dw30"}
+        holds = {5: "g_woven0", 6: "dw20", 7: "g_woven0"}
         for j in range(1, TILES):
             scatter_vector(j, 0)
             if 3 <= j <= 5:

@@ -36,7 +36,7 @@ def tile_attend_gds_sq_kernel(tc, xT, wT, v_words, v_scales, wt, xm, offs, out):
         ps = ctx.enter_context(tc.psum_pool(name="ps", bufs=1))
 
         def tile(name, shape, dtype, tag=None):
-            return sb.tile(shape, dtype, name=name, tag=tag or name, align_bytes=64)
+            return sb.tile(shape, dtype, name=name, tag=tag or name, align_bytes=256)
 
         offsets = sb.tile([P, N // 16], U16, name="offsets")
         halves = [slice(h * HALF, (h + 1) * HALF) for h in range(2)]

@@ -265,7 +265,8 @@ def tile_attend_gds_sq_kernel(tc, xT, wT, v_words, v_scales, wt, xm, offs, out):
         for q in range(2):
             part_words(q)
             close_scores(q)
-        gather_words(2, 2)
+        gather_words(2, 1)
+        gather_words(3, 1)
         for c in range(5):
             xm_weave(c, nc.scalar.copy)
         part_words(2)

@@ -26,7 +26,7 @@ TILES = D // P
 WINDOWS = 5
 QUARTERS = N // P
 HALF = N // 2
-XM_WIDTHS = (256, 128, 128, 128, 384)
+XM_WIDTHS = (256, 128, 128, 128, 128, 256)
 
 
 def tile_attend_gds_sq_kernel(tc, xT, wT, v_words, v_scales, wt, xm, offs, out):
@@ -50,11 +50,10 @@ def tile_attend_gds_sq_kernel(tc, xT, wT, v_words, v_scales, wt, xm, offs, out):
         v_planes = tile("v_planes", [P, PASSES, N], U8)
         nc.vector.memset(v_planes[:].rearrange("p o t -> p (o t)").bitcast(I32), 0)
 
-        w_first, w_last = tile("w_first", [P, T], F32), tile("w_last", [P, T], F32)
-        w_three = [tile(f"w_three{g}", [P, PACK - 1, T], F32) for g in range(PASSES)]
+        w_early, w_three, w_last = tile("w_early", [P, PACK, T], F32), tile("w_three", [P, PACK - 1, T], F32), tile("w_last", [P, T], F32)
         w_raw = [
-            [w_first[:]] + [w_three[0][:, t, :] for t in range(PACK - 1)],
-            [w_three[1][:, t, :] for t in range(PACK - 1)] + [w_last[:]],
+            [w_early[:, t, :] for t in range(PACK)],
+            [w_three[:, t, :] for t in range(PACK - 1)] + [w_last[:]],
         ]
         w_rows = [wT[g * K_PASS : (g + 1) * K_PASS, :].rearrange("(p t) c -> p t c", t=PACK) for g in range(PASSES)]
         x_raw = [tile("x_raw0", [P, PACK, R], F32)]
@@ -62,11 +61,10 @@ def tile_attend_gds_sq_kernel(tc, xT, wT, v_words, v_scales, wt, xm, offs, out):
         wt_sb = tile("wt_sb", [P, PACK], F32)
         v_raw = tile("v_raw", [P, T], U32)
 
-        nc.sync.dma_start(out=w_first[:], in_=w_rows[0][:, 0, :])
+        nc.sync.dma_start(out=w_early[:], in_=w_rows[0])
         nc.sync.dma_start(offsets[:], offs)
         nc.sync.dma_start(out=v_bytes[0:P:8, :, :].bitcast(I32), in_=v_scales.rearrange("o f t -> f o t").bitcast(I32))
-        nc.sync.dma_start(out=w_three[0][:], in_=w_rows[0][:, 1:, :])
-        nc.sync.dma_start(out=w_three[1][:], in_=w_rows[1][:, : PACK - 1, :])
+        nc.sync.dma_start(out=w_three[:], in_=w_rows[1][:, : PACK - 1, :])
         nc.sync.dma_start(out=w_last[:], in_=w_rows[1][:, PACK - 1, :])
         nc.sync.dma_start(out=x_raw[0][:], in_=x_rows[0])
         v_picked = tile("v_picked", [P, PASSES, N], U8)
@@ -109,7 +107,7 @@ def tile_attend_gds_sq_kernel(tc, xT, wT, v_words, v_scales, wt, xm, offs, out):
             planes = tile(f"w_planes{g}", [P, PACK, N], F32)
             woven = [tile(f"w_woven{g}{h}", [P, HALF, PACK], BF16) for h in range(2)]
             for t in range(PACK):
-                if g == PASSES - 1 and t in (0, PACK - 1):
+                if t == 0 or g * PACK + t == TILES - 1:
                     nc.vector.tensor_copy(planes[:, t, :], w_raw[g][t].indirect(offsets[:]))
                 else:
                     nc.scalar.activation(planes[:, t, :], w_raw[g][t].indirect(offsets[:]), COPY)

from contextlib import ExitStack

import concourse.mybir as mybir

N, T, D, R = 512, 2048, 1024, 512
FLOPS = 3 * 2 * R * D * N

F32 = mybir.dt.float32
BF16 = mybir.dt.bfloat16
I32 = mybir.dt.int32
U32 = mybir.dt.uint32
U16 = mybir.dt.uint16
U8 = mybir.dt.uint8
E4M3 = mybir.dt.float8_e4m3fn_x4
E5M2 = mybir.dt.float8_e5m2_x4
E2M1 = mybir.dt.float4_e2m1fn_x4
COPY = mybir.ActivationFunctionType.Copy
MULT = mybir.AluOpType.mult
ADD = mybir.AluOpType.add

P = 128
PACK = 4
K_PASS = P * PACK
PASSES = D // K_PASS
TILES = D // P
WINDOWS = 5
QUARTERS = N // P
HALF = N // 2
XM_WIDTHS = (256, 128, 128, 128, 128, 256)


def tile_attend_gds_sq_kernel(tc, xT, wT, v_words, v_scales, wt, xm, offs, out):
    nc = tc.nc
    with ExitStack() as ctx:
        sb = ctx.enter_context(tc.tile_pool(name="sb", bufs=1))
        ps = ctx.enter_context(tc.psum_pool(name="ps", bufs=1))

        def tile(name, shape, dtype, tag=None):
            return sb.tile(shape, dtype, name=name, tag=tag or name, align_bytes=256)

        offsets = sb.tile([P, N // 16], U16, name="offsets")
        halves = [slice(h * HALF, (h + 1) * HALF) for h in range(2)]
        quarters = [slice(q * P, (q + 1) * P) for q in range(QUARTERS)]

        def entries(slots):
            return offsets[:, slots.start // 16 : slots.stop // 16]

        v_bytes = tile("v_bytes", [P, PASSES, T], U8)
        nc.vector.memset(v_bytes[:].rearrange("p o t -> p (o t)").bitcast(I32), 0)
        v_planes = tile("v_planes", [P, PASSES, N], U8)
        nc.vector.memset(v_planes[:].rearrange("p o t -> p (o t)").bitcast(I32), 0)

        w_early, w_three, w_last = tile("w_early", [P, PACK, T], F32), tile("w_three", [P, PACK - 1, T], F32), tile("w_last", [P, T], F32)
        w_raw = [
            [w_early[:, t, :] for t in range(PACK)],
            [w_three[:, t, :] for t in range(PACK - 1)] + [w_last[:]],
        ]
        w_rows = [wT[g * K_PASS : (g + 1) * K_PASS, :].rearrange("(p t) c -> p t c", t=PACK) for g in range(PASSES)]
        x_raw = [tile("x_raw0", [P, PACK, R], F32)]
        x_rows = [xT[0, g * K_PASS : (g + 1) * K_PASS, :].rearrange("(p t) r -> p t r", t=PACK) for g in range(PASSES)]
        wt_sb = tile("wt_sb", [P, PACK], F32)
        v_raw = tile("v_raw", [P, T], U32)

        nc.sync.dma_start(out=w_early[:], in_=w_rows[0])
        nc.sync.dma_start(offsets[:], offs)
        nc.sync.dma_start(out=v_bytes[0:P:8, :, :].bitcast(I32), in_=v_scales.rearrange("o f t -> f o t").bitcast(I32))
        nc.sync.dma_start(out=w_three[:], in_=w_rows[1][:, : PACK - 1, :])
        nc.sync.dma_start(out=w_last[:], in_=w_rows[1][:, PACK - 1, :])
        nc.sync.dma_start(out=x_raw[0][:], in_=x_rows[0])
        v_picked = tile("v_picked", [P, PASSES, N], U8)
        for o in range(PASSES):
            nc.vector.tensor_copy(v_picked[:, o, :], v_bytes[:, o, :].indirect(offsets[:]))
        for q in range(0, P, 32):
            nc.sync.dma_start(out=v_planes[q : q + 4, :, :].bitcast(I32), in_=v_picked[q : q + 32 : 8, :, :].bitcast(I32))
        x_raw.append(tile("x_raw1", [P, PACK, R], F32, tag="v_bytes"))
        nc.sync.dma_start(out=x_raw[1][:], in_=x_rows[1])
        nc.sync.dma_start(out=v_raw[:].bitcast(I32), in_=v_words[0].rearrange("p t b -> p (t b)").bitcast(I32))
        nc.sync.dma_start(out=wt_sb[:], in_=wt[0].rearrange("(p t) o -> p (t o)", t=PACK))
        xm_rows = xm[0].rearrange("(p t) d -> p t d", t=PACK)
        xm_raw = []
        for c, width in enumerate(XM_WIDTHS):
            first = sum(XM_WIDTHS[:c])
            xm_raw.append(tile(f"xm_raw{c}", [P, PACK, width], F32))
            nc.sync.dma_start(out=xm_raw[c][:], in_=xm_rows[:, :, first : first + width])

        def weave_views(dst, src):
            return (
                dst.rearrange("p (c i) t -> p c t i", i=4),
                src.rearrange("p t (c i) -> p c t i", i=4),
            )

        def deal_views(woven, raw, first, count):
            return (
                woven.rearrange("p r (c e) t -> p c t e r", e=2),
                raw.rearrange("p t (c e r) -> p c t e r", e=2, r=PACK)[:, :, :, :, first : first + count],
            )

        def quantize(name, woven, width, fmt, tag=None):
            codes = tile(f"{name}_codes", [P, width], U32, tag=tag)
            scales = tile(f"{name}_scales", [P, width], U8)
            nc.vector.quantize_mx(codes[:].bitcast(fmt), scales[:], woven)
            return codes, scales

        w = []
        windows = [tile(f"window{j}", [P, T], F32) for j in range(WINDOWS)]
        for g in range(PASSES):
            planes = tile(f"w_planes{g}", [P, PACK, N], F32)
            woven = [tile(f"w_woven{g}{h}", [P, HALF, PACK], BF16) for h in range(2)]
            for t in range(PACK):
                if t == 0 or g * PACK + t == TILES - 1:
                    nc.vector.tensor_copy(planes[:, t, :], w_raw[g][t].indirect(offsets[:]))
                else:
                    nc.scalar.activation(planes[:, t, :], w_raw[g][t].indirect(offsets[:]), COPY)
                if 0 < g * PACK + t <= WINDOWS:
                    nc.vector.memset(windows[g * PACK + t - 1][:].bitcast(I32), 0)
            nc.scalar.activation(*weave_views(woven[0][:], planes[:, :, halves[0]]), COPY, scale=-1.0)
            nc.vector.tensor_scalar_mul(*weave_views(woven[1][:], planes[:, :, halves[1]]), -1.0)
            w.append(woven)

        def deal(g):
            woven = [tile(f"x{g}{u}_woven", [P, 2, P, PACK], BF16) for u in range(2)]
            nc.vector.tensor_copy(*deal_views(woven[0][:], x_raw[g][:], 0, 2))
            nc.scalar.copy(*deal_views(woven[1][:], x_raw[g][:], 2, 2))
            return woven

        def quantize_w(g, tags):
            return [quantize(f"w{g}{h}", w[g][h][:].rearrange("p n t -> p (n t)"), HALF, E4M3, tag=tags[h]) for h in range(2)]

        def quantize_rows(g, woven):
            return [quantize(f"x{g}{u}", woven[u][:].rearrange("p r s t -> p (r s t)"), 2 * P, E4M3) for u in range(2)]

        scores = [ps.tile([P, PACK, P], F32, name=f"scores{q}", tag=f"scores{q}") for q in range(QUARTERS)]

        def score_pass(q, r, x, rhs, rhs_scale, start=False, stop=False):
            codes, scales = x[r // 2]
            nc.tensor.matmul_mx(
                scores[q][:, r, :],
                lhsT=codes[:, quarters[r % 2]].bitcast(E4M3),
                lhsT_scale=scales[:, quarters[r % 2]],
                rhs=rhs,
                rhs_scale=rhs_scale,
                start=start,
                stop=stop,
            )

        x = []
        for g in range(PASSES):
            w_q = quantize_w(g, ("x00_woven", "x01_woven") if g else (None, None))
            x.append(quantize_rows(g, deal(g)))
            for q in range(QUARTERS):
                codes, scales = w_q[q // 2]
                for r in range(PACK):
                    score_pass(q, r, x[g], codes[:, quarters[q % 2]].bitcast(E4M3), scales[:, quarters[q % 2]], start=g == 0 and r == 0)

        v_pairs = {}

        def gather_words(first, count):
            pairs = tile(f"v_pairs{first}", [P, count * P], U32, tag=f"v_pairs{first % 2}")
            nc.vector.tensor_copy(pairs[:], v_raw[:].indirect(entries(slice(first * P, (first + count) * P))))
            for q in range(count):
                v_pairs[first + q] = pairs[:, q * P : (q + 1) * P]

        v_codes = {}

        def part_words(q):
            codes = tile(f"v_codes{q}", [P, PASSES, 2 * P], U8, tag=f"v_codes{q % 3}")
            nc.vector.tensor_copy(
                codes[:].rearrange("p o b -> p (o b)").bitcast(U16).rearrange("p (o n) -> p o n", o=PASSES),
                v_pairs[q].bitcast(U16).rearrange("p (n o) -> p o n", o=PASSES),
            )
            v_codes[q] = codes

        def close_scores(q):
            for o in range(PASSES):
                for r in range(PACK):
                    score_pass(q, r, x[o], v_codes[q][:, o, :].bitcast(E2M1), v_planes[:, o, quarters[q]], stop=o == PASSES - 1 and r == PACK - 1)

        xm_woven, xm_q = {}, {}
        xm_cols = [raw[:, :, m : m + P] for raw, width in zip(xm_raw, XM_WIDTHS) for m in range(0, width, P)]

        def xm_weave(c, copy, tag=None):
            xm_woven[c] = tile(f"xm_woven{c}", [P, P, PACK], BF16, tag=tag)
            copy(*weave_views(xm_woven[c][:], xm_cols[c]))

        def weave_gpsimd(dst, src):
            nc.gpsimd.tensor_scalar(dst, src, 1.0, 0.0, MULT, ADD)

        def xm_quantize(c, tag=None):
            codes, scales = quantize(f"xm{c}", xm_woven[c][:].rearrange("p d t -> p (d t)"), P, E4M3, tag=tag)
            xm_q[c] = codes[:], scales[:]

        g_woven = [tile(f"g_woven{q}", [P, P, PACK], BF16, tag=f"g_woven{q % 2}") for q in range(QUARTERS)]
        g_codes = tile("g_codes", [P, N], U32)
        g_scales = tile("g_scales", [P, N], U8)
        wt_rows = wt_sb[:].unsqueeze(1).to_broadcast([P, P, PACK])

        def weigh(q):
            nc.vector.tensor_tensor(g_woven[q][:], scores[q][:].rearrange("p r n -> p n r"), wt_rows, MULT)

        def quantize_g(q):
            nc.vector.quantize_mx(
                g_codes[:, quarters[q]].bitcast(E5M2), g_scales[:, quarters[q]], g_woven[q][:].rearrange("p n t -> p (n t)")
            )

        dws = {}

        def bank_tile(name, tag):
            return ps.tile([P, N], F32, name=name, tag=tag)

        def gradient(j, slots, target):
            codes, scales = xm_q[j]
            nc.tensor.matmul_mx(
                target,
                lhsT=codes.bitcast(E4M3),
                lhsT_scale=scales,
                rhs=g_codes[:, slots].bitcast(E5M2),
                rhs_scale=g_scales[:, slots],
                start=True,
                stop=True,
            )
            return target

        def empty_scalar(j, h, source):
            dws[j, h] = tile(f"dw{j}{h}", [P, HALF], F32)[:]
            nc.scalar.activation(dws[j, h], source, COPY, scale=-1.0)

        def empty_vector(j, h, source, tag=None):
            dws[j, h] = tile(f"dw{j}{h}", [P, HALF], F32, tag=tag)[:]
            nc.vector.tensor_scalar_mul(dws[j, h], source, -1.0)

        def window(j, h):
            return windows[j % WINDOWS][:].indirect(entries(halves[h]))

        def scatter_scalar(j, h):
            nc.scalar.activation(window(j, h), dws[j, h], COPY)

        def scatter_vector(j, h):
            nc.vector.tensor_copy(window(j, h), dws[j, h])

        def store(j):
            nc.sync.dma_start(out=out[j * P : (j + 1) * P, :], in_=windows[j % WINDOWS][:])

        tags = [f"grad{b}" for b in range(4)] + [f"scores{q}" for q in range(QUARTERS)]
        first, shared = (bank_tile(f"early{b}", tags[b]) for b in range(2))

        def half(j, h):
            bank = bank_tile(f"half{j}{h}", tags[2 * j + h - 1])
            (empty_scalar if h else empty_vector)(j, h, gradient(j, halves[h], bank[:, halves[0]]))

        def whole(j):
            bank = bank_tile(f"whole{j}", tags[3 if j == 4 else (j + 3) % len(tags)])
            gradient(j, slice(0, N), bank[:])
            if j % 2:
                empty_vector(j, 0, bank[:, halves[0]], tag="dw30")
                empty_scalar(j, 1, bank[:, halves[1]])
            else:
                dw = tile(f"dw{j}", [P, N], F32)
                nc.scalar.activation(dw[:], bank[:], COPY, scale=-1.0)
                dws[j, 0], dws[j, 1] = dw[:, halves[0]], dw[:, halves[1]]

        gather_words(0, 1)
        gather_words(1, 1)
        for q in range(2):
            part_words(q)
            close_scores(q)
        gather_words(2, 1)
        gather_words(3, 1)
        for c in range(5):
            xm_weave(c, nc.scalar.copy)
        part_words(2)
        weigh(0)
        part_words(3)
        weigh(1)
        xm_quantize(0, tag="v_pairs0")
        dws[0, 0] = tile("dw00", [P, HALF], F32)[:]
        for q, bank in enumerate((first, bank_tile("early_second", "scores0"))):
            quantize_g(q)
            nc.scalar.activation(dws[0, 0][:, quarters[q]], gradient(0, quarters[q], bank[:, quarters[0]]), COPY, scale=-1.0)
        scatter_scalar(0, 0)
        for q in range(2, QUARTERS):
            close_scores(q)
        xm_quantize(1, tag="v_codes1")
        second = gradient(1, halves[0], bank_tile("half10", "scores1")[:, halves[0]])
        for q in range(2, QUARTERS):
            weigh(q)
        dws[0, 1] = tile("dw01", [P, HALF], F32)[:]
        for q, bank in enumerate((shared, bank_tile("early_last", "scores2"))):
            quantize_g(2 + q)
            nc.vector.tensor_scalar_mul(dws[0, 1][:, quarters[q]], gradient(0, quarters[2 + q], bank[:, quarters[0]]), -1.0)
        empty_vector(1, 0, second, tag="g_woven0")
        xm_quantize(2, tag="v_codes0")
        xm_quantize(3, tag="g_woven1")
        xm_quantize(4, tag="xm_woven3")
        half(1, 1)
        scatter_scalar(0, 1)
        store(0)
        holds = {5: "g_woven0", 6: "dw20", 7: "g_woven0"}
        for j in range(1, TILES):
            scatter_vector(j, 0)
            if 3 <= j <= 5:
                xm_quantize(j + 2)
            if j <= 2:
                for h in range(2):
                    half(j + 1, h)
            elif j + 1 < TILES:
                whole(j + 1)
            if 2 <= j <= 4:
                xm_weave(j + 3, weave_gpsimd, tag=holds[j + 3])
            scatter_scalar(j, 1)
            store(j)
